import numpy as np
import ml_dtypes


def mxq(x, axis, fmt="e4m3"):
    dtype, down = {"e4m3": (ml_dtypes.float8_e4m3fn, 7), "e5m2": (ml_dtypes.float8_e5m2, 14)}[fmt]
    v = np.moveaxis(np.asarray(x, np.float32).astype(ml_dtypes.bfloat16).astype(np.float64), axis, -1)
    blocks = v.reshape(v.shape[:-1] + (-1, 32))
    amax = np.abs(blocks).max(-1, keepdims=True)
    byte = np.maximum(np.where(amax > 0, np.frexp(amax)[1] - 1 + 127, 0) - down, 1)
    scale = np.exp2(byte - 127.0)
    codes = (blocks / scale).astype(np.float32).astype(dtype).astype(np.float64)
    return np.moveaxis((codes * scale).reshape(v.shape), -1, axis)


WIDE = False


def mx_kscale(k):
    if not WIDE:
        return np.ones(k)
    levels = np.array([10, -10, 5, -5, 0])
    if k % 512:
        return np.exp2(np.random.permutation(np.resize(levels, k // 32))).repeat(32)
    a = np.empty((k // 512, 16))
    for p in range(k // 512):
        a[p, :8] = np.random.permutation(np.resize(levels, 8))
        for g in range(8):
            far = levels[np.abs(levels - a[p, g]) >= 10]
            a[p, g + 8] = far[np.random.randint(len(far))]
    return np.exp2(a.ravel()).repeat(32)


BF16 = ml_dtypes.bfloat16


def bf(x):
    return np.asarray(x, np.float32).astype(BF16)


def f64(x):
    return np.asarray(x).astype(np.float64)


E2M1 = np.array([0.0, 0.5, 1.0, 1.5, 2.0, 3.0, 4.0, 6.0, -0.0, -0.5, -1.0, -1.5, -2.0, -3.0, -4.0, -6.0])


def pack_weight(w, fmt):
    k, n = w.shape
    w = f64(bf(w)).reshape(k // 32, 32, n)
    amax = np.abs(w).max(1)
    if fmt == "e4m3":
        byte = np.frexp(amax)[1] - 1 + 127 - 7
    else:
        mant, ex = np.frexp(amax / 6.0)
        byte = np.where(mant > 0.5, ex, ex - 1) + 127
    byte = np.clip(np.where(amax > 0, byte, 1), 1, 254)
    scaled = (w * np.exp2(127.0 - byte)[:, None, :]).reshape(k, n).astype(np.float32)
    by_word = np.ascontiguousarray(scaled.reshape(k // 512, 128, 4, n).transpose(0, 1, 3, 2))
    if fmt == "e4m3":
        words = by_word.astype(ml_dtypes.float8_e4m3fn).view(np.uint8)
    else:
        c = by_word.astype(ml_dtypes.float4_e2m1fn).view(np.uint8) & 0xF
        words = c[..., 0::2] | (c[..., 1::2] << 4)
    return np.ascontiguousarray(words), np.ascontiguousarray(byte.astype(np.uint8).reshape(k // 512, 16, n))


def unpack_weight(words, scales, fmt):
    g, p, n, _ = words.shape
    if fmt == "e4m3":
        vals = np.ascontiguousarray(words).view(ml_dtypes.float8_e4m3fn).astype(np.float64)
    else:
        nib = np.empty((g, p, n, 4), np.uint8)
        nib[..., 0::2] = words & 0xF
        nib[..., 1::2] = words >> 4
        vals = E2M1[nib]
    vals = vals * np.repeat(np.exp2(scales.astype(np.float64) - 127.0), 8, axis=1)[..., None]
    return vals.transpose(0, 1, 3, 2).reshape(g * 512, n)
def pack4(w):
    words, scales = pack_weight(w, "e2m1")
    return words.reshape(words.shape[0], 128, -1), scales


def unpack4(words, scales):
    return unpack_weight(words.reshape(words.shape[0], 128, -1, 2), scales, "e2m1")


def planes(Y):
    n, m = Y.shape
    b = f64(bf(Y)).reshape(n // 32, 32, m)
    amax = np.abs(b).max(1)
    byte = np.clip(np.where(amax > 0, np.frexp(amax)[1] - 1 + 127 - 7, 1), 1, 254)
    codes = (b * np.exp2(127.0 - byte)[:, None, :]).reshape(n, m).astype(np.float32).astype(ml_dtypes.float8_e4m3fn).view(np.uint8)
    words = codes.reshape(n // 512, 128, 4, m).transpose(0, 1, 3, 2)
    return np.ascontiguousarray(words), np.ascontiguousarray(byte.astype(np.uint8).reshape(n // 512, 16, m))


T, G, P = 1024, 1024, 1024

HEBB = 0.03125


def setup_inputs():
    sg, sp, st = mx_kscale(G), mx_kscale(P), mx_kscale(T)
    g = np.random.standard_normal((T, G)) * sg
    wg = np.random.standard_normal((G, P)) / np.sqrt(G) / sg[:, None]
    wg_words, wg_scales = pack4(wg)
    x = np.random.standard_normal((T, P))
    q = np.random.standard_normal((T, P)) * sp
    m0 = np.random.standard_normal((P, P)) / np.sqrt(P) / sp[:, None]
    s = (1.0 + 0.1 * np.random.standard_normal(T)) * st
    c = (1.0 + 0.1 * np.random.standard_normal(T)) / st
    return {"g": bf(g), "wg_words": wg_words, "wg_scales": wg_scales, "x": bf(x), "q": bf(q), "m0": bf(m0), "s": bf(s), "c": bf(c)}


def _place_code(g, wg_words, wg_scales, x):
    gt = mxq(f64(g), 1, "e4m3") @ unpack4(wg_words, wg_scales)
    return np.minimum(np.maximum(gt * f64(x), -1.0), 1.0)


def _retrieved_code(q, m0):
    return np.tanh(mxq(f64(q), 1, "e4m3") @ mxq(f64(m0), 0, "e4m3"))


def core(g, wg_words, wg_scales, x, q, m0, s, c):
    p = _place_code(g, wg_words, wg_scales, x)
    ph = _retrieved_code(q, m0)
    l = f64(s)[:, None] * (p - ph)
    r = f64(c)[:, None] * (p + ph)
    return HEBB * (mxq(l.T, 1, "e4m3") @ mxq(r, 0, "e4m3"))


def reference(g, wg_words, wg_scales, x, q, m0, s, c):
    R_out = core(g, wg_words, wg_scales, x, q, m0, s, c)
    words, scales = planes(R_out.T)
    return R_out, words, scales

@@ -1,0 +1,554 @@
+from contextlib import ExitStack
+
+import concourse.mybir as mybir
+from concourse.masks import make_identity
+
+N = 1024
+HEBB = 0.03125
+FLOPS = 3 * 2 * N * N * N
+
+F32 = mybir.dt.float32
+BF16 = mybir.dt.bfloat16
+U32 = mybir.dt.uint32
+I32 = mybir.dt.int32
+U8 = mybir.dt.uint8
+FP8 = mybir.dt.float8_e4m3fn_x4
+FP4 = mybir.dt.float4_e2m1fn_x4
+ALU = mybir.AluOpType
+ACT = mybir.ActivationFunctionType
+
+V = 0
+S = 1
+SC_BUFS = {"sp": 1, "sph": 2, "cp": 1, "cph": 1}
+
+
+def tile_differencesumouterproduct_kernel(tc, g, wg_words, wg_scales, x, q, m0, s, c, out_0, out_1, out_2):
+    nc = tc.nc
+    with ExitStack() as ctx:
+        keep = ctx.enter_context(tc.tile_pool(name="keep", bufs=1))
+        raw = ctx.enter_context(tc.tile_pool(name="raw", bufs=1))
+        work = ctx.enter_context(tc.tile_pool(name="work", bufs=1))
+        psum = ctx.enter_context(tc.psum_pool(name="psum", bufs=1))
+
+        ident = keep.tile([128, 128], F32, name="ident")
+        wgw = [keep.tile([128, 2, 1024], U8, name=f"wgw{h}", align_bytes=64) for h in range(2)]
+        wgs = keep.tile([128, 2, 1024], U8, name="wgs", align_bytes=64)
+        s_raw = keep.tile([128, 8], BF16, name="s_raw")
+        c_raw = keep.tile([128, 8], BF16, name="c_raw")
+        s_sb = keep.tile([128, 8], F32, name="s_sb")
+        c_sb = keep.tile([128, 8], F32, name="c_sb")
+        warm = keep.tile([128, 1], F32, name="warm")
+        act_codes = {}
+        act_scales = {}
+        for mat in ("g", "q"):
+            for tg in range(2):
+                act_codes[mat, tg] = keep.tile([128, 4, 2, 128], U32, name=f"{mat}{tg}_codes", align_bytes=64)
+                act_scales[mat, tg] = keep.tile([128, 4, 2, 128], U8, name=f"{mat}{tg}_scales", align_bytes=64)
+        m_codes = keep.tile([128, 2, N], U32, name="m_codes", align_bytes=64)
+        m_scales = keep.tile([128, 2, N], U8, name="m_scales", align_bytes=64)
+        l_codes = keep.tile([128, 2, N], U32, name="l_codes", align_bytes=64)
+        l_scales = keep.tile([128, 2, N], U8, name="l_scales", align_bytes=64)
+        r_codes = keep.tile([128, 2, N], U32, name="r_codes", align_bytes=64)
+        r_scales = keep.tile([128, 2, N], U8, name="r_scales", align_bytes=64)
+
+        nc.vector.memset(warm[:], 0.0)
+        nc.gpsimd.memset(wgs[:].rearrange("p g n -> p (g n)").bitcast(I32), 0)
+        make_identity(nc, ident[:])
+        nc.scalar.activation(out=warm[:], in_=warm[:], func=ACT.Tanh)
+
+        raws = {}
+
+        def load_m0(h):
+            t = raw.tile([128, 2, 4, 512], BF16, name=f"m0_{h}", tag="raw8k", bufs=3)
+            raws["m", h] = t
+            src = m0.rearrange("(g p j) n -> g p j n", g=2, j=4)
+            for gk in range(2):
+                nc.sync.dma_start(out=t[:, gk], in_=src[gk, :, :, h * 512 : (h + 1) * 512])
+
+        def load_act(mat, tg):
+            t = raw.tile([128, 4, 1024], BF16, name=f"{mat}_{tg}", tag="raw8k", bufs=3)
+            raws[mat, tg] = t
+            src = (g if mat == "g" else q).rearrange("(tg m t) k -> tg m t k", tg=2, t=4)
+            for half in range(2):
+                nc.sync.dma_start(out=t[:, 2 * half : 2 * half + 2], in_=src[tg, :, 2 * half : 2 * half + 2, :])
+
+        def load_x(tg, h):
+            t = raw.tile([128, 4, 512], BF16, name=f"x_{tg}{h}", tag="x", bufs=4)
+            raws["x", tg, h] = t
+            src = x.rearrange("(tg m t) n -> tg m t n", tg=2, t=4)
+            nc.sync.dma_start(out=t[:], in_=src[tg, :, :, h * 512 : (h + 1) * 512])
+
+        def load_wg(h):
+            nc.sync.dma_start(
+                out=wgw[h][:].bitcast(I32),
+                in_=wg_words[:, :, h * 1024 : (h + 1) * 1024].rearrange("g p b -> p g b").bitcast(I32),
+            )
+
+        for Q in range(4):
+            nc.gpsimd.dma_start(
+                out=wgs[32 * Q : 32 * Q + 4].bitcast(I32),
+                in_=wg_scales[:, 4 * Q : 4 * Q + 4, :].rearrange("g r n -> r g n").bitcast(I32),
+            )
+        for vec, rt in ((s, s_raw), (c, c_raw)):
+            nc.gpsimd.dma_start(
+                out=rt[:].rearrange("p (a t) -> p a t", a=2),
+                in_=vec.rearrange("(a p t) -> p a t", a=2, t=4),
+            )
+        load_m0(0)
+        load_act("q", 0)
+        load_act("g", 0)
+        load_wg(0)
+        load_x(0, 0)
+        load_act("g", 1)
+        load_act("q", 1)
+        load_x(1, 0)
+        load_m0(1)
+        load_wg(1)
+        load_x(0, 1)
+        load_x(1, 1)
+
+        def bank(tag):
+            return psum.tile([128, 512], F32, name="bank_" + tag, tag=tag, bufs={"t": 3, "s": 2, "v": 3}[tag])
+
+        il = {}
+
+        G = 2
+
+        def m0_il(h, gk, eng):
+            t = work.tile([128, 2048], BF16, name=f"m_il{h}{gk}", tag="il", bufs=4, align_bytes=64)
+            il["m", h, gk] = t
+            o = t[:].rearrange("p (c i j) -> p c j i", i=4, j=4)
+            i = raws["m", h][:, gk].rearrange("p j (c i) -> p c j i", i=4)
+            if eng == V:
+                nc.vector.tensor_copy(out=o, in_=i)
+            elif eng == G:
+                nc.gpsimd.tensor_scalar(out=o, in0=i, scalar1=1.0, scalar2=0.0, op0=ALU.mult, op1=ALU.add)
+            else:
+                nc.scalar.copy(out=o, in_=i)
+
+        def m0_quant(h, gk):
+            nc.vector.quantize_mx(
+                out=m_codes[:, gk, h * 512 : (h + 1) * 512].bitcast(FP8),
+                scales=m_scales[:, gk, h * 512 : (h + 1) * 512],
+                in_=il["m", h, gk][:],
+            )
+
+        def turn(mat, tg, ts, eng):
+            b = bank("t")
+            words = raws[mat, tg][:, ts, :].bitcast(F32)
+            for gk in range(2):
+                for u in range(2):
+                    k = 2 * gk + u
+                    nc.tensor.transpose(
+                        b[:, k * 128 : (k + 1) * 128], words[:, 256 * gk + u : 256 * (gk + 1) : 2], ident[:]
+                    )
+            if ts % 2 == 0:
+                il[mat, tg, ts // 2] = work.tile(
+                    [128, 2048], BF16, name=f"{mat}_il{tg}{ts}", tag="il", bufs=4, align_bytes=64
+                )
+            o = il[mat, tg, ts // 2][:].bitcast(F32)[:, (ts % 2) * 512 : (ts % 2 + 1) * 512]
+            o = o.rearrange("p (g m u) -> p g m u", g=2, u=2)
+            i = b[:].rearrange("p (g u m) -> p g m u", g=2, u=2)
+            if eng == V:
+                nc.vector.tensor_copy(out=o, in_=i)
+            else:
+                nc.scalar.copy(out=o, in_=i)
+
+        def act_quant(mat, tg, pair):
+            nc.vector.quantize_mx(
+                out=act_codes[mat, tg][:, 2 * pair : 2 * pair + 2].rearrange("p a b c -> p (a b c)").bitcast(FP8),
+                scales=act_scales[mat, tg][:, 2 * pair : 2 * pair + 2].rearrange("p a b c -> p (a b c)"),
+                in_=il[mat, tg, pair][:],
+            )
+
+        chunks = ((0, 0), (1, 0), (0, 1), (1, 1))
+        gt_bank = {}
+        ph_bank = {}
+
+        def mm_gt(k, ts):
+            tg, h = chunks[k]
+            b = bank("v")
+            gt_bank[k, ts] = b
+            for gk in range(2):
+                nc.tensor.matmul_mx(
+                    out=b[:],
+                    lhsT=act_codes["g", tg][:, ts, gk, :].bitcast(FP8),
+                    lhsT_scale=act_scales["g", tg][:, ts, gk, :],
+                    rhs=wgw[h][:, gk, :].bitcast(FP4),
+                    rhs_scale=wgs[:, gk, h * 512 : (h + 1) * 512],
+                    start=(gk == 0),
+                    stop=(gk == 1),
+                )
+
+        def mm_ph(k, ts):
+            tg, h = chunks[k]
+            b = bank("s")
+            ph_bank[k, ts] = b
+            for gk in range(2):
+                nc.tensor.matmul_mx(
+                    out=b[:],
+                    lhsT=act_codes["q", tg][:, ts, gk, :].bitcast(FP8),
+                    lhsT_scale=act_scales["q", tg][:, ts, gk, :],
+                    rhs=m_codes[:, gk, h * 512 : (h + 1) * 512].bitcast(FP8),
+                    rhs_scale=m_scales[:, gk, h * 512 : (h + 1) * 512],
+                    start=(gk == 0),
+                    stop=(gk == 1),
+                )
+
+        pt = {}
+
+        def y(k, ts):
+            tg, h = chunks[k]
+            if ts == 0:
+                pt["p", k] = work.tile([128, 4, 512], F32, name=f"p{k}", tag="p", bufs=2)
+            nc.vector.tensor_tensor(
+                out=pt["p", k][:, ts, :], in0=gt_bank[k, ts][:], in1=raws["x", tg, h][:, ts, :], op=ALU.mult
+            )
+
+        def clamp(k, lo=0, hi=4, eng=V):
+            t = pt["p", k][:, lo:hi]
+            (nc.gpsimd if eng == G else nc.vector).tensor_scalar(
+                out=t, in0=t, scalar1=1.0, scalar2=-1.0, op0=ALU.min, op1=ALU.max
+            )
+
+        def tanh(k, ts):
+            if ts == 0:
+                pt["ph", k] = work.tile([128, 4, 512], F32, name=f"ph{k}", tag="ph", bufs=2)
+            nc.scalar.activation(out=pt["ph", k][:, ts, :], in_=ph_bank[k, ts][:], func=ACT.Tanh)
+
+        def scale(k, vec, src, ts=None):
+            tg, h = chunks[k]
+            key = vec + src
+            if ts is None:
+                for t4 in range(4):
+                    scale(k, vec, src, t4)
+                return
+            if ts == 0:
+                pt[key, k] = work.tile([128, 4, 512], F32, name=f"{key}{k}", tag=key, bufs=SC_BUFS[key])
+            v = s_sb if vec == "s" else c_sb
+            nc.scalar.activation(
+                out=pt[key, k][:, ts, :],
+                in_=pt[src, k][:, ts, :],
+                func=ACT.Copy,
+                scale=v[:, tg * 4 + ts : tg * 4 + ts + 1],
+            )
+
+        def r_view(o):
+            return o.rearrange("p (b m) t -> p m t b", b=4)
+
+        def r_src(i):
+            return i.rearrange("p t (m b) -> p m t b", b=4)
+
+        def r_join(k):
+            t = work.tile([128, 512, 4], BF16, name=f"r{k}", tag="r", bufs=1, align_bytes=64)
+            pt["r", k] = t
+            nc.vector.tensor_tensor(
+                out=r_view(t[:]), in0=r_src(pt["cp", k][:]), in1=r_src(pt["cph", k][:]), op=ALU.add
+            )
+
+        def e_sum(k):
+            e = work.tile([128, 512, 4], F32, name=f"e{k}", tag="e", bufs=1)
+            pt["e", k] = e
+            nc.vector.tensor_tensor(
+                out=e[:].rearrange("p (b m) t -> p m t b", b=4),
+                in0=pt["p", k][:].rearrange("p t (m b) -> p m t b", b=4),
+                in1=pt["ph", k][:].rearrange("p t (m b) -> p m t b", b=4),
+                op=ALU.add,
+            )
+
+        def r_mul(k):
+            tg, h = chunks[k]
+            t = work.tile([128, 512, 4], BF16, name=f"r{k}", tag="r", bufs=1, align_bytes=64)
+            pt["r", k] = t
+            nc.vector.tensor_tensor(
+                out=t[:],
+                in0=pt["e", k][:],
+                in1=c_sb[:, tg * 4 : tg * 4 + 4].unsqueeze(1).to_broadcast([128, 512, 4]),
+                op=ALU.mult,
+            )
+
+        def l_diff(k):
+            t = work.tile([128, 512, 4], BF16, name=f"l{k}", tag="l", bufs=1, align_bytes=64)
+            pt["l", k] = t
+            nc.vector.tensor_tensor(
+                out=t[:].rearrange("p (c i) t -> p c t i", i=4),
+                in0=pt["sp", k][:].rearrange("p t (c i) -> p c t i", i=4),
+                in1=pt["sph", k][:].rearrange("p t (c i) -> p c t i", i=4),
+                op=ALU.subtract,
+            )
+
+        def lr_quant(k, which):
+            tg, h = chunks[k]
+            codes, scales = (l_codes, l_scales) if which == "l" else (r_codes, r_scales)
+            nc.vector.quantize_mx(
+                out=codes[:, tg, h * 512 : (h + 1) * 512].bitcast(FP8),
+                scales=scales[:, tg, h * 512 : (h + 1) * 512],
+                in_=pt[which, k][:].rearrange("p n t -> p (n t)"),
+            )
+
+        L = (l_codes, l_scales)
+        R = (r_codes, r_scales)
+
+        def mx(out, stat, scol, mov, mcol, width, tgs):
+            for tg in tgs:
+                nc.tensor.matmul_mx(
+                    out=out,
+                    lhsT=stat[0][:, tg, scol : scol + 128].bitcast(FP8),
+                    lhsT_scale=stat[1][:, tg, scol : scol + 128],
+                    rhs=mov[0][:, tg, mcol : mcol + width].bitcast(FP8),
+                    rhs_scale=mov[1][:, tg, mcol : mcol + width],
+                    start=(tg == 0),
+                    stop=(tg == 1),
+                )
+
+        def copy_scaled(o, i, eng):
+            if eng == V:
+                nc.vector.tensor_scalar(out=o, in0=i, scalar1=HEBB, scalar2=None, op0=ALU.mult)
+            else:
+                nc.scalar.activation(out=o, in_=i, func=ACT.Copy, scale=HEBB)
+
+        ob = {}
+        o_sb = {}
+
+        def out_first(i, h, tag):
+            ob[i, h] = bank(tag)
+            mx(ob[i, h][:], L, i * 128, R, h * 512, 512, (0,))
+
+        def out_second(i, h):
+            mx(ob[i, h][:], L, i * 128, R, h * 512, 512, (1,))
+
+        def out_mm(i, h, tag):
+            out_first(i, h, tag)
+            out_second(i, h)
+
+        def out_copy(i, h, eng):
+            o = work.tile([128, 512], F32, name=f"o{i}{h}", tag="o", bufs=6)
+            o_sb[i, h] = o
+            copy_scaled(
+                o[:].rearrange("p (m b) -> p m b", b=4), ob[i, h][:].rearrange("p (b m) -> p m b", b=4), eng
+            )
+            nc.sync.dma_start(out=out_0[i * 128 : (i + 1) * 128, h * 512 : (h + 1) * 512], in_=o[:])
+
+        planes = {}
+
+        def plane_tile(gb, ah):
+            if (gb, ah) not in planes:
+                planes[gb, ah] = work.tile([128, 512, 4], BF16, name=f"pb{gb}{ah}", tag="pb", bufs=2, align_bytes=64)
+            return planes[gb, ah]
+
+        def outT_mm(gb, j, tag):
+            b = bank(tag)
+            ob["T", gb, j] = b
+            for tb in range(4):
+                mx(b[:, tb * 128 : (tb + 1) * 128], R, gb * 512 + tb * 128, L, j * 128, 128, (0, 1))
+
+        def outT_copy(gb, j, eng):
+            copy_scaled(
+                plane_tile(gb, j // 4)[:, (j % 4) * 128 : (j % 4 + 1) * 128, :],
+                ob["T", gb, j][:].rearrange("p (b a) -> p a b", b=4),
+                eng,
+            )
+
+        o16 = {}
+
+        def conv(i, h, eng):
+            t = work.tile([128, 512], BF16, name=f"o16_{i}{h}", tag="o16", bufs=2)
+            o16[i, h] = t
+            if eng == G:
+                nc.gpsimd.tensor_scalar(out=t[:], in0=o_sb[i, h][:], scalar1=1.0, scalar2=0.0, op0=ALU.mult, op1=ALU.add)
+            elif eng == V:
+                nc.vector.tensor_copy(out=t[:], in_=o_sb[i, h][:])
+            else:
+                nc.scalar.copy(out=t[:], in_=o_sb[i, h][:])
+
+        def plane_turn(gb, pair, tag):
+            b = bank(tag)
+            ob["P", gb, pair] = b
+            for ii in range(2):
+                words = o16[2 * pair + ii, gb][:].bitcast(F32)
+                for u in range(2):
+                    kk = 2 * ii + u
+                    nc.tensor.transpose(b[:, kk * 128 : (kk + 1) * 128], words[:, u:256:2], ident[:])
+
+        def plane_copy(gb, pair, eng):
+            ah = pair // 2
+            t = plane_tile(gb, ah)[:].rearrange("p a t -> p (a t)").bitcast(F32)
+            o = t[:, (pair % 2) * 512 : (pair % 2 + 1) * 512].rearrange("p (i a u) -> p i a u", i=2, u=2)
+            i = ob["P", gb, pair][:].rearrange("p (i u a) -> p i a u", i=2, u=2)
+            if eng == V:
+                nc.vector.tensor_copy(out=o, in_=i)
+            else:
+                nc.scalar.copy(out=o, in_=i)
+
+        pl_scales = [keep.tile([128, N], U8, name=f"pl_scales{gb}", align_bytes=64) for gb in range(2)]
+
+        def plane_quant(gb, ah):
+            w = work.tile([128, 512], U32, name=f"pw{gb}{ah}", tag=f"pw{gb}{ah}", bufs=1, align_bytes=64)
+            nc.vector.quantize_mx(
+                out=w[:].bitcast(FP8),
+                scales=pl_scales[gb][:, ah * 512 : (ah + 1) * 512],
+                in_=planes[gb, ah][:].rearrange("p a t -> p (a t)"),
+            )
+            nc.sync.dma_start(
+                out=out_1[gb].rearrange("p a t -> p (a t)")[:, ah * 2048 : (ah + 1) * 2048].bitcast(I32),
+                in_=w[:].bitcast(I32),
+            )
+            for Q in range(4):
+                nc.sync.dma_start(
+                    out=out_2[gb, 4 * Q : 4 * Q + 4, ah * 512 : (ah + 1) * 512].bitcast(I32),
+                    in_=pl_scales[gb][32 * Q : 32 * Q + 4, ah * 512 : (ah + 1) * 512].bitcast(I32),
+                )
+
+        m0_il(0, 0, V)
+        m0_il(0, 1, V)
+        m0_quant(0, 0)
+        for ts in range(4):
+            turn("q", 0, ts, S)
+        m0_quant(0, 1)
+        act_quant("q", 0, 0)
+        act_quant("q", 0, 1)
+        turn("g", 0, 0, S)
+        turn("g", 0, 1, S)
+        turn("g", 0, 2, S)
+        turn("g", 0, 3, S)
+        for ts in range(2):
+            mm_ph(0, ts)
+            tanh(0, ts)
+        act_quant("g", 0, 0)
+        act_quant("g", 0, 1)
+        nc.vector.tensor_copy(out=s_sb[:], in_=s_raw[:])
+        for ts in range(2):
+            mm_gt(0, ts)
+            y(0, ts)
+        for ts in range(2, 4):
+            mm_ph(0, ts)
+            tanh(0, ts)
+        for ts in range(2, 4):
+            mm_gt(0, ts)
+            y(0, ts)
+        for ts in range(4):
+            scale(0, "s", "ph", ts)
+        nc.vector.tensor_copy(out=c_sb[:], in_=c_raw[:])
+        clamp(0)
+
+        for ts in range(4):
+            turn("g", 1, ts, S)
+        for ts in range(4):
+            scale(0, "s", "p", ts)
+        e_sum(0)
+        act_quant("g", 1, 0)
+        act_quant("g", 1, 1)
+        for ts in range(4):
+            turn("q", 1, ts, S)
+        r_mul(0)
+        for ts in range(4):
+            mm_gt(1, ts)
+            y(1, ts)
+            if ts == 1:
+                lr_quant(0, "r")
+                act_quant("q", 1, 0)
+        act_quant("q", 1, 1)
+        for ts in range(4):
+            mm_ph(1, ts)
+            tanh(1, ts)
+        l_diff(0)
+        clamp(1)
+        m0_il(1, 0, S)
+        m0_il(1, 1, S)
+        for ts in range(4):
+            scale(1, "s", "ph", ts)
+        lr_quant(0, "l")
+        for ts in range(4):
+            scale(1, "s", "p", ts)
+        m0_quant(1, 0)
+        m0_quant(1, 1)
+        for ts in range(4):
+            scale(1, "c", "ph", ts)
+        for ts in range(4):
+            scale(1, "c", "p", ts)
+
+        for ts in range(4):
+            mm_gt(2, ts)
+            mm_ph(2, ts)
+            y(2, ts)
+            tanh(2, ts)
+        l_diff(1)
+        clamp(2)
+        for ts in range(4):
+            scale(2, "s", "ph", ts)
+        r_join(1)
+        lr_quant(1, "l")
+        lr_quant(1, "r")
+        for ts in range(4):
+            scale(2, "s", "p", ts)
+        e_sum(2)
+        for i in range(3):
+            out_mm(i, 0, "t")
+        out_copy(0, 0, V)
+        out_copy(1, 0, S)
+        out_copy(2, 0, S)
+        r_mul(2)
+
+        for ts in range(4):
+            mm_gt(3, ts)
+            mm_ph(3, ts)
+            y(3, ts)
+            tanh(3, ts)
+            if ts == 1:
+                lr_quant(2, "r")
+        out_mm(3, 0, "t")
+        outT_mm(0, 0, "t")
+        outT_mm(0, 1, "t")
+        outT_mm(0, 2, "s")
+        outT_mm(0, 3, "s")
+        out_copy(3, 0, S)
+        l_diff(2)
+        clamp(3)
+        for ts in range(4):
+            scale(3, "s", "ph", ts)
+        outT_copy(0, 0, S)
+        lr_quant(2, "l")
+        for i in range(3):
+            out_first(4 + i, 0, "v")
+        for ts in range(4):
+            scale(3, "s", "p", ts)
+        e_sum(3)
+        outT_copy(0, 1, S)
+        outT_copy(0, 2, S)
+        outT_copy(0, 3, V)
+        r_mul(3)
+        plane_quant(0, 0)
+        lr_quant(3, "r")
+        l_diff(3)
+
+        tags = ["t", "s", "t", "s", "t"]
+        seq = [("o", i, 1) for i in range(4)] + [("T", 1, j) for j in range(4)]
+        for n, (kind, a, b) in enumerate(seq):
+            if kind == "o":
+                out_mm(a, b, tags[n % 5])
+                out_copy(a, b, S)
+            else:
+                outT_mm(a, b, tags[n % 5])
+                outT_copy(a, b, S if b < 2 else V)
+            if n == 5:
+                lr_quant(3, "l")
+        out_second(4, 0)
+        out_second(5, 0)
+        out_second(6, 0)
+        out_copy(4, 0, V)
+        out_copy(5, 0, S)
+        out_copy(6, 0, V)
+        plane_quant(1, 0)
+        tags = ["v", "v", "v", "t", "s", "t", "s", "t"]
+        seq = [("o", 7, 0)] + [("T", 0, j) for j in range(4, 8)]
+        seq += [("o", i, 1) for i in range(4, 8)] + [("T", 1, j) for j in range(4, 8)]
+        for n, (kind, a, b) in enumerate(seq):
+            eng = S if n % 2 == 0 else V
+            if kind == "o":
+                out_mm(a, b, tags[n % 8])
+                out_copy(a, b, eng)
+            else:
+                outT_mm(a, b, tags[n % 8])
+                outT_copy(a, b, eng)
+                if b % 4 == 3:
+                    plane_quant(a, b // 4)

@@ -19,7 +19,8 @@ ACT = mybir.ActivationFunctionType
 
 V = 0
 S = 1
-SC_BUFS = {"sp": 1, "sph": 2, "cp": 1, "cph": 1}
+M0_PIECES = 1
+TINY = 2.0**-100
 
 
 def tile_differencesumouterproduct_kernel(tc, g, wg_words, wg_scales, x, q, m0, s, c, out_0, out_1, out_2):
@@ -29,6 +30,7 @@ def tile_differencesumouterproduct_kernel(tc, g, wg_words, wg_scales, x, q, m0, 
         raw = ctx.enter_context(tc.tile_pool(name="raw", bufs=1))
         work = ctx.enter_context(tc.tile_pool(name="work", bufs=1))
         psum = ctx.enter_context(tc.psum_pool(name="psum", bufs=1))
+        ctx.enter_context(tc.manual_schedule())
 
         ident = keep.tile([128, 128], F32, name="ident")
         wgw = [keep.tile([128, 2, 1024], U8, name=f"wgw{h}", align_bytes=64) for h in range(2)]
@@ -37,6 +39,11 @@ def tile_differencesumouterproduct_kernel(tc, g, wg_words, wg_scales, x, q, m0, 
         c_raw = keep.tile([128, 8], BF16, name="c_raw")
         s_sb = keep.tile([128, 8], F32, name="s_sb")
         c_sb = keep.tile([128, 8], F32, name="c_sb")
+        is0 = keep.tile([128, 8], F32, name="is0")
+        neg = keep.tile([128, 8], F32, name="neg")
+        hi = keep.tile([128, 8], F32, name="hi")
+        lo = keep.tile([128, 8], F32, name="lo")
+        rho = keep.tile([128, 8], F32, name="rho")
         warm = keep.tile([128, 1], F32, name="warm")
         act_codes = {}
         act_scales = {}
@@ -51,6 +58,11 @@ def tile_differencesumouterproduct_kernel(tc, g, wg_words, wg_scales, x, q, m0, 
         r_codes = keep.tile([128, 2, N], U32, name="r_codes", align_bytes=64)
         r_scales = keep.tile([128, 2, N], U8, name="r_scales", align_bytes=64)
 
+        for vec, rt in ((s, s_raw), (c, c_raw)):
+            nc.scalar.dma_start(
+                out=rt[:].rearrange("p (a t) -> p a t", a=2),
+                in_=vec.rearrange("(a p t) -> p a t", a=2, t=4),
+            )
         nc.vector.memset(warm[:], 0.0)
         nc.gpsimd.memset(wgs[:].rearrange("p g n -> p (g n)").bitcast(I32), 0)
         make_identity(nc, ident[:])
@@ -59,18 +71,24 @@ def tile_differencesumouterproduct_kernel(tc, g, wg_words, wg_scales, x, q, m0, 
         raws = {}
 
         def load_m0(h):
-            t = raw.tile([128, 2, 4, 512], BF16, name=f"m0_{h}", tag="raw8k", bufs=3)
+            t = raw.tile([128, 2, 4, 512], BF16, name=f"m0_{h}", tag="raw8k", bufs=4)
             raws["m", h] = t
             src = m0.rearrange("(g p j) n -> g p j n", g=2, j=4)
             for gk in range(2):
-                nc.sync.dma_start(out=t[:, gk], in_=src[gk, :, :, h * 512 : (h + 1) * 512])
+                for piece in range(M0_PIECES if h == 0 and gk == 0 else 1):
+                    w = 512 // (M0_PIECES if h == 0 and gk == 0 else 1)
+                    nc.sync.dma_start(
+                        out=t[:, gk, :, piece * w : (piece + 1) * w],
+                        in_=src[gk, :, :, h * 512 + piece * w : h * 512 + (piece + 1) * w],
+                    )
 
-        def load_act(mat, tg):
-            t = raw.tile([128, 4, 1024], BF16, name=f"{mat}_{tg}", tag="raw8k", bufs=3)
+        def load_act(mat, tg, parts=2):
+            t = raw.tile([128, 4, 1024], BF16, name=f"{mat}_{tg}", tag="raw8k", bufs=4)
             raws[mat, tg] = t
             src = (g if mat == "g" else q).rearrange("(tg m t) k -> tg m t k", tg=2, t=4)
-            for half in range(2):
-                nc.sync.dma_start(out=t[:, 2 * half : 2 * half + 2], in_=src[tg, :, 2 * half : 2 * half + 2, :])
+            step = 4 // parts
+            for a in range(0, 4, step):
+                nc.sync.dma_start(out=t[:, a : a + step], in_=src[tg, :, a : a + step, :])
 
         def load_x(tg, h):
             t = raw.tile([128, 4, 512], BF16, name=f"x_{tg}{h}", tag="x", bufs=4)
@@ -89,14 +107,9 @@ def tile_differencesumouterproduct_kernel(tc, g, wg_words, wg_scales, x, q, m0, 
                 out=wgs[32 * Q : 32 * Q + 4].bitcast(I32),
                 in_=wg_scales[:, 4 * Q : 4 * Q + 4, :].rearrange("g r n -> r g n").bitcast(I32),
             )
-        for vec, rt in ((s, s_raw), (c, c_raw)):
-            nc.gpsimd.dma_start(
-                out=rt[:].rearrange("p (a t) -> p a t", a=2),
-                in_=vec.rearrange("(a p t) -> p a t", a=2, t=4),
-            )
         load_m0(0)
-        load_act("q", 0)
-        load_act("g", 0)
+        load_act("q", 0, 4)
+        load_act("g", 0, 4)
         load_wg(0)
         load_x(0, 0)
         load_act("g", 1)
@@ -114,11 +127,12 @@ def tile_differencesumouterproduct_kernel(tc, g, wg_words, wg_scales, x, q, m0, 
 
         G = 2
 
-        def m0_il(h, gk, eng):
-            t = work.tile([128, 2048], BF16, name=f"m_il{h}{gk}", tag="il", bufs=4, align_bytes=64)
-            il["m", h, gk] = t
-            o = t[:].rearrange("p (c i j) -> p c j i", i=4, j=4)
-            i = raws["m", h][:, gk].rearrange("p j (c i) -> p c j i", i=4)
+        def m0_il(h, gk, eng, lo=0, hi=512):
+            if ("m", h, gk) not in il:
+                il["m", h, gk] = work.tile([128, 2048], BF16, name=f"m_il{h}{gk}", tag="il", bufs=5, align_bytes=64)
+            t = il["m", h, gk]
+            o = t[:, 4 * lo : 4 * hi].rearrange("p (c i j) -> p c j i", i=4, j=4)
+            i = raws["m", h][:, gk, :, lo:hi].rearrange("p j (c i) -> p c j i", i=4)
             if eng == V:
                 nc.vector.tensor_copy(out=o, in_=i)
             elif eng == G:
@@ -133,8 +147,11 @@ def tile_differencesumouterproduct_kernel(tc, g, wg_words, wg_scales, x, q, m0, 
                 in_=il["m", h, gk][:],
             )
 
-        def turn(mat, tg, ts, eng):
+        turned = {}
+
+        def turn_mm(mat, tg, ts):
             b = bank("t")
+            turned[mat, tg, ts] = b
             words = raws[mat, tg][:, ts, :].bitcast(F32)
             for gk in range(2):
                 for u in range(2):
@@ -142,9 +159,12 @@ def tile_differencesumouterproduct_kernel(tc, g, wg_words, wg_scales, x, q, m0, 
                     nc.tensor.transpose(
                         b[:, k * 128 : (k + 1) * 128], words[:, 256 * gk + u : 256 * (gk + 1) : 2], ident[:]
                     )
-            if ts % 2 == 0:
+
+        def turn_copy(mat, tg, ts, eng):
+            b = turned[mat, tg, ts]
+            if (mat, tg, ts // 2) not in il:
                 il[mat, tg, ts // 2] = work.tile(
-                    [128, 2048], BF16, name=f"{mat}_il{tg}{ts}", tag="il", bufs=4, align_bytes=64
+                    [128, 2048], BF16, name=f"{mat}_il{tg}{ts}", tag="il", bufs=5, align_bytes=64
                 )
             o = il[mat, tg, ts // 2][:].bitcast(F32)[:, (ts % 2) * 512 : (ts % 2 + 1) * 512]
             o = o.rearrange("p (g m u) -> p g m u", g=2, u=2)
@@ -199,33 +219,55 @@ def tile_differencesumouterproduct_kernel(tc, g, wg_words, wg_scales, x, q, m0, 
 
         def y(k, ts):
             tg, h = chunks[k]
-            if ts == 0:
+            if ("p", k) not in pt:
                 pt["p", k] = work.tile([128, 4, 512], F32, name=f"p{k}", tag="p", bufs=2)
-            nc.vector.tensor_tensor(
-                out=pt["p", k][:, ts, :], in0=gt_bank[k, ts][:], in1=raws["x", tg, h][:, ts, :], op=ALU.mult
+            nc.vector.scalar_tensor_tensor(
+                out=pt["p", k][:, ts, :],
+                in0=gt_bank[k, ts][:],
+                scalar=s_sb[:, tg * 4 + ts : tg * 4 + ts + 1],
+                in1=raws["x", tg, h][:, ts, :],
+                op0=ALU.mult,
+                op1=ALU.mult,
             )
 
-        def clamp(k, lo=0, hi=4, eng=V):
-            t = pt["p", k][:, lo:hi]
+        def clamp(k, ts, eng=V):
+            tg, h = chunks[k]
+            t = pt["p", k][:, ts]
+            col = tg * 4 + ts
             (nc.gpsimd if eng == G else nc.vector).tensor_scalar(
-                out=t, in0=t, scalar1=1.0, scalar2=-1.0, op0=ALU.min, op1=ALU.max
+                out=t,
+                in0=t,
+                scalar1=hi[:, col : col + 1],
+                scalar2=lo[:, col : col + 1],
+                op0=ALU.min,
+                op1=ALU.max,
             )
+
+        def prep():
+            nc.vector.tensor_copy(out=s_sb[:], in_=s_raw[:])
+            nc.vector.tensor_copy(out=c_sb[:], in_=c_raw[:])
+            nc.vector.tensor_scalar(out=is0[:], in0=s_sb[:], scalar1=0.0, scalar2=TINY, op0=ALU.is_equal, op1=ALU.mult)
+            nc.vector.tensor_tensor(out=s_sb[:], in0=s_sb[:], in1=is0[:], op=ALU.add)
+            nc.vector.tensor_scalar(out=neg[:], in0=s_sb[:], scalar1=-1.0, scalar2=None, op0=ALU.mult)
+            nc.vector.reciprocal(out=rho[:], in_=s_sb[:])
+            nc.vector.tensor_tensor(out=hi[:], in0=s_sb[:], in1=neg[:], op=ALU.max)
+            nc.vector.tensor_tensor(out=rho[:], in0=rho[:], in1=c_sb[:], op=ALU.mult)
+            nc.vector.tensor_tensor(out=lo[:], in0=s_sb[:], in1=neg[:], op=ALU.min)
 
         def tanh(k, ts):
-            if ts == 0:
+            if ("ph", k) not in pt:
                 pt["ph", k] = work.tile([128, 4, 512], F32, name=f"ph{k}", tag="ph", bufs=2)
             nc.scalar.activation(out=pt["ph", k][:, ts, :], in_=ph_bank[k, ts][:], func=ACT.Tanh)
 
-        def scale(k, vec, src, ts=None):
+        def scale(k, key, src, ts=None):
             tg, h = chunks[k]
-            key = vec + src
             if ts is None:
                 for t4 in range(4):
-                    scale(k, vec, src, t4)
+                    scale(k, key, src, t4)
                 return
-            if ts == 0:
-                pt[key, k] = work.tile([128, 4, 512], F32, name=f"{key}{k}", tag=key, bufs=SC_BUFS[key])
-            v = s_sb if vec == "s" else c_sb
+            if (key, k) not in pt:
+                pt[key, k] = work.tile([128, 4, 512], F32, name=f"{key}{k}", tag=key, bufs=1)
+            v = s_sb if key == src else rho
             nc.scalar.activation(
                 out=pt[key, k][:, ts, :],
                 in_=pt[src, k][:, ts, :],
@@ -263,27 +305,28 @@ def tile_differencesumouterproduct_kernel(tc, g, wg_words, wg_scales, x, q, m0, 
             nc.vector.tensor_tensor(
                 out=t[:],
                 in0=pt["e", k][:],
-                in1=c_sb[:, tg * 4 : tg * 4 + 4].unsqueeze(1).to_broadcast([128, 512, 4]),
+                in1=rho[:, tg * 4 : tg * 4 + 4].unsqueeze(1).to_broadcast([128, 512, 4]),
                 op=ALU.mult,
             )
 
-        def l_diff(k):
-            t = work.tile([128, 512, 4], BF16, name=f"l{k}", tag="l", bufs=1, align_bytes=64)
-            pt["l", k] = t
+        def l_diff(k, lo=0, hi=512):
+            if ("l", k) not in pt:
+                pt["l", k] = work.tile([128, 512, 4], BF16, name=f"l{k}", tag="l", bufs=1, align_bytes=64)
+            t = pt["l", k]
             nc.vector.tensor_tensor(
-                out=t[:].rearrange("p (c i) t -> p c t i", i=4),
-                in0=pt["sp", k][:].rearrange("p t (c i) -> p c t i", i=4),
-                in1=pt["sph", k][:].rearrange("p t (c i) -> p c t i", i=4),
+                out=t[:, lo:hi].rearrange("p (c i) t -> p c t i", i=4),
+                in0=pt["p", k][:, :, lo:hi].rearrange("p t (c i) -> p c t i", i=4),
+                in1=pt["ph", k][:, :, lo:hi].rearrange("p t (c i) -> p c t i", i=4),
                 op=ALU.subtract,
             )
 
-        def lr_quant(k, which):
+        def lr_quant(k, which, lo=0, hi=512):
             tg, h = chunks[k]
             codes, scales = (l_codes, l_scales) if which == "l" else (r_codes, r_scales)
             nc.vector.quantize_mx(
-                out=codes[:, tg, h * 512 : (h + 1) * 512].bitcast(FP8),
-                scales=scales[:, tg, h * 512 : (h + 1) * 512],
-                in_=pt[which, k][:].rearrange("p n t -> p (n t)"),
+                out=codes[:, tg, h * 512 + lo : h * 512 + hi].bitcast(FP8),
+                scales=scales[:, tg, h * 512 + lo : h * 512 + hi],
+                in_=pt[which, k][:, lo:hi].rearrange("p n t -> p (n t)"),
             )
 
         L = (l_codes, l_scales)
@@ -322,7 +365,7 @@ def tile_differencesumouterproduct_kernel(tc, g, wg_words, wg_scales, x, q, m0, 
             out_second(i, h)
 
         def out_copy(i, h, eng):
-            o = work.tile([128, 512], F32, name=f"o{i}{h}", tag="o", bufs=6)
+            o = work.tile([128, 512], F32, name=f"o{i}{h}", tag="o", bufs=9)
             o_sb[i, h] = o
             copy_scaled(
                 o[:].rearrange("p (m b) -> p m b", b=4), ob[i, h][:].rearrange("p (b m) -> p m b", b=4), eng
@@ -352,7 +395,7 @@ def tile_differencesumouterproduct_kernel(tc, g, wg_words, wg_scales, x, q, m0, 
         o16 = {}
 
         def conv(i, h, eng):
-            t = work.tile([128, 512], BF16, name=f"o16_{i}{h}", tag="o16", bufs=2)
+            t = work.tile([128, 512], BF16, name=f"o16_{i}{h}", tag="o16", bufs=4)
             o16[i, h] = t
             if eng == G:
                 nc.gpsimd.tensor_scalar(out=t[:], in0=o_sb[i, h][:], scalar1=1.0, scalar2=0.0, op0=ALU.mult, op1=ALU.add)
@@ -399,156 +442,260 @@ def tile_differencesumouterproduct_kernel(tc, g, wg_words, wg_scales, x, q, m0, 
                     in_=pl_scales[gb][32 * Q : 32 * Q + 4, ah * 512 : (ah + 1) * 512].bitcast(I32),
                 )
 
-        m0_il(0, 0, V)
         m0_il(0, 1, V)
-        m0_quant(0, 0)
-        for ts in range(4):
-            turn("q", 0, ts, S)
         m0_quant(0, 1)
+        prep()
+        m0_il(0, 0, S)
+        turn_mm("q", 0, 0)
+        turn_copy("q", 0, 0, S)
+        turn_mm("q", 0, 1)
+        turn_copy("q", 0, 1, S)
+        turn_mm("q", 0, 3)
+        turn_copy("q", 0, 3, S)
+        turn_mm("g", 0, 0)
+        m0_quant(0, 0)
+        turn_mm("q", 0, 2)
+        turn_copy("q", 0, 2, V)
+        turn_copy("g", 0, 0, S)
+        turn_mm("g", 0, 1)
+        turn_copy("g", 0, 1, S)
         act_quant("q", 0, 0)
+        turn_mm("g", 0, 2)
+        turn_copy("g", 0, 2, S)
         act_quant("q", 0, 1)
-        turn("g", 0, 0, S)
-        turn("g", 0, 1, S)
-        turn("g", 0, 2, S)
-        turn("g", 0, 3, S)
-        for ts in range(2):
-            mm_ph(0, ts)
-            tanh(0, ts)
         act_quant("g", 0, 0)
+        turn_mm("g", 0, 3)
+        turn_copy("g", 0, 3, V)
+        mm_ph(0, 0)
         act_quant("g", 0, 1)
-        nc.vector.tensor_copy(out=s_sb[:], in_=s_raw[:])
-        for ts in range(2):
-            mm_gt(0, ts)
-            y(0, ts)
-        for ts in range(2, 4):
-            mm_ph(0, ts)
-            tanh(0, ts)
-        for ts in range(2, 4):
-            mm_gt(0, ts)
-            y(0, ts)
-        for ts in range(4):
-            scale(0, "s", "ph", ts)
-        nc.vector.tensor_copy(out=c_sb[:], in_=c_raw[:])
-        clamp(0)
-
-        for ts in range(4):
-            turn("g", 1, ts, S)
-        for ts in range(4):
-            scale(0, "s", "p", ts)
+        tanh(0, 0)
+        mm_ph(0, 1)
+        tanh(0, 1)
+        scale(0, "ph", "ph", 1)
+        mm_gt(0, 0)
+        y(0, 0)
+        mm_ph(0, 2)
+        scale(0, "ph", "ph", 0)
+        clamp(0, 0)
+        mm_gt(0, 1)
+        mm_ph(0, 3)
+        y(0, 1)
+        mm_gt(0, 2)
+        y(0, 2)
+        mm_gt(0, 3)
+        tanh(0, 2)
+        scale(0, "ph", "ph", 2)
+        turn_mm("g", 1, 0)
+        tanh(0, 3)
+        scale(0, "ph", "ph", 3)
+        turn_mm("g", 1, 1)
+        turn_mm("g", 1, 2)
+        turn_mm("g", 1, 3)
+        turn_copy("g", 1, 0, S)
+        y(0, 3)
+        clamp(0, 2)
+        clamp(0, 3)
+        clamp(0, 1)
+        turn_mm("q", 1, 0)
         e_sum(0)
-        act_quant("g", 1, 0)
-        act_quant("g", 1, 1)
-        for ts in range(4):
-            turn("q", 1, ts, S)
-        r_mul(0)
-        for ts in range(4):
-            mm_gt(1, ts)
-            y(1, ts)
-            if ts == 1:
-                lr_quant(0, "r")
-                act_quant("q", 1, 0)
-        act_quant("q", 1, 1)
-        for ts in range(4):
-            mm_ph(1, ts)
-            tanh(1, ts)
-        l_diff(0)
-        clamp(1)
-        m0_il(1, 0, S)
+        turn_copy("g", 1, 1, S)
+        turn_copy("g", 1, 2, S)
+        turn_copy("g", 1, 3, S)
+        turn_copy("q", 1, 0, S)
+        turn_mm("q", 1, 1)
         m0_il(1, 1, S)
-        for ts in range(4):
-            scale(1, "s", "ph", ts)
-        lr_quant(0, "l")
-        for ts in range(4):
-            scale(1, "s", "p", ts)
-        m0_quant(1, 0)
+        turn_mm("q", 1, 3)
+        turn_copy("q", 1, 3, S)
+        act_quant("g", 1, 0)
+        mm_gt(1, 1)
+        turn_mm("q", 1, 2)
+        r_mul(0)
+        act_quant("g", 1, 1)
+        mm_gt(1, 0)
+        y(1, 0)
+        mm_gt(1, 2)
+        mm_gt(1, 3)
+        mm_gt(2, 0)
+        turn_copy("q", 1, 1, S)
+        y(1, 1)
+        y(1, 2)
+        act_quant("q", 1, 0)
+        mm_ph(1, 0)
+        turn_copy("q", 1, 2, S)
+        mm_gt(2, 1)
+        clamp(1, 1)
+        m0_il(1, 0, S)
+        scale(1, "cp", "p", 1)
+        y(1, 3)
+        lr_quant(0, "r")
+        clamp(1, 0)
+        tanh(1, 0)
+        mm_ph(1, 1)
+        act_quant("q", 1, 1)
+        mm_ph(1, 2)
+        mm_ph(1, 3)
+        tanh(1, 1)
+        clamp(1, 2)
+        scale(1, "ph", "ph", 0)
+        scale(1, "ph", "ph", 1)
+        mm_gt(2, 2)
+        scale(1, "cp", "p", 0)
+        tanh(1, 2)
+        l_diff(0)
+        tanh(1, 3)
+        scale(1, "cph", "ph", 1)
+        scale(1, "ph", "ph", 3)
+        scale(1, "ph", "ph", 2)
+        clamp(1, 3)
+        scale(1, "cp", "p", 3)
+        scale(1, "cph", "ph", 0)
+        mm_gt(2, 3)
         m0_quant(1, 1)
-        for ts in range(4):
-            scale(1, "c", "ph", ts)
-        for ts in range(4):
-            scale(1, "c", "p", ts)
-
-        for ts in range(4):
-            mm_gt(2, ts)
-            mm_ph(2, ts)
-            y(2, ts)
-            tanh(2, ts)
+        m0_quant(1, 0)
+        mm_ph(2, 1)
+        tanh(2, 1)
+        y(2, 0)
+        scale(1, "cph", "ph", 2)
+        scale(1, "cph", "ph", 3)
+        mm_ph(2, 0)
+        tanh(2, 0)
+        y(2, 2)
+        lr_quant(0, "l")
+        clamp(2, 0)
+        scale(1, "cp", "p", 2)
+        mm_gt(3, 2)
+        mm_ph(2, 2)
+        tanh(2, 2)
+        mm_ph(2, 3)
+        tanh(2, 3)
+        y(2, 1)
+        scale(2, "ph", "ph", 0)
         l_diff(1)
-        clamp(2)
-        for ts in range(4):
-            scale(2, "s", "ph", ts)
+        mm_ph(3, 0)
+        y(2, 3)
         r_join(1)
-        lr_quant(1, "l")
+        scale(2, "ph", "ph", 3)
+        scale(2, "ph", "ph", 2)
+        mm_ph(3, 1)
+        mm_gt(3, 0)
+        mm_ph(3, 2)
+        scale(2, "ph", "ph", 1)
+        tanh(3, 0)
+        clamp(2, 3)
+        clamp(2, 1)
+        scale(2, "cp", "p", 1)
+        scale(2, "cph", "ph", 2)
         lr_quant(1, "r")
-        for ts in range(4):
-            scale(2, "s", "p", ts)
-        e_sum(2)
-        for i in range(3):
-            out_mm(i, 0, "t")
+        tanh(3, 2)
+        clamp(2, 2)
+        lr_quant(1, "l")
+        scale(2, "cph", "ph", 0)
+        scale(2, "cp", "p", 0)
+        y(3, 0)
+        scale(2, "cph", "ph", 3)
+        out_mm(0, 0, "t")
         out_copy(0, 0, V)
+        y(3, 2)
+        scale(2, "cp", "p", 3)
+        out_mm(1, 0, "t")
+        out_mm(2, 0, "t")
+        out_copy(2, 0, V)
+        scale(2, "cp", "p", 2)
         out_copy(1, 0, S)
-        out_copy(2, 0, S)
-        r_mul(2)
-
-        for ts in range(4):
-            mm_gt(3, ts)
-            mm_ph(3, ts)
-            y(3, ts)
-            tanh(3, ts)
-            if ts == 1:
-                lr_quant(2, "r")
-        out_mm(3, 0, "t")
+        scale(2, "cph", "ph", 1)
+        mm_gt(3, 1)
+        y(3, 1)
+        tanh(3, 1)
         outT_mm(0, 0, "t")
-        outT_mm(0, 1, "t")
-        outT_mm(0, 2, "s")
+        outT_copy(0, 0, V)
+        scale(3, "ph", "ph", 2)
+        mm_gt(3, 3)
+        scale(3, "ph", "ph", 0)
+        y(3, 3)
+        scale(3, "ph", "ph", 1)
+        mm_ph(3, 3)
+        tanh(3, 3)
         outT_mm(0, 3, "s")
-        out_copy(3, 0, S)
+        scale(3, "cph", "ph", 2)
+        clamp(3, 2)
+        clamp(3, 1)
+        clamp(3, 3)
+        scale(3, "cp", "p", 3)
+        r_join(2)
+        clamp(3, 0)
+        scale(3, "ph", "ph", 3)
+        outT_mm(0, 1, "t")
         l_diff(2)
-        clamp(3)
-        for ts in range(4):
-            scale(3, "s", "ph", ts)
-        outT_copy(0, 0, S)
         lr_quant(2, "l")
-        for i in range(3):
-            out_first(4 + i, 0, "v")
-        for ts in range(4):
-            scale(3, "s", "p", ts)
-        e_sum(3)
-        outT_copy(0, 1, S)
+        scale(3, "cph", "ph", 0)
+        scale(3, "cph", "ph", 3)
+        scale(3, "cp", "p", 0)
+        scale(3, "cp", "p", 2)
+        scale(3, "cp", "p", 1)
+        out_first(4, 0, "v")
+        out_first(5, 0, "v")
+        scale(3, "cph", "ph", 1)
+        lr_quant(2, "r")
+        out_mm(3, 0, "t")
+        out_copy(3, 0, S)
+        outT_mm(0, 2, "s")
         outT_copy(0, 2, S)
-        outT_copy(0, 3, V)
-        r_mul(3)
-        plane_quant(0, 0)
-        lr_quant(3, "r")
         l_diff(3)
-
-        tags = ["t", "s", "t", "s", "t"]
-        seq = [("o", i, 1) for i in range(4)] + [("T", 1, j) for j in range(4)]
-        for n, (kind, a, b) in enumerate(seq):
-            if kind == "o":
-                out_mm(a, b, tags[n % 5])
-                out_copy(a, b, S)
-            else:
-                outT_mm(a, b, tags[n % 5])
-                outT_copy(a, b, S if b < 2 else V)
-            if n == 5:
-                lr_quant(3, "l")
-        out_second(4, 0)
-        out_second(5, 0)
+        r_join(3)
+        lr_quant(3, "r")
+        outT_copy(0, 1, S)
+        out_first(6, 0, "v")
+        outT_copy(0, 3, S)
+        plane_quant(0, 0)
+        lr_quant(3, "l")
+        out_mm(0, 1, "t")
+        out_copy(0, 1, S)
+        out_mm(1, 1, "s")
+        out_copy(1, 1, V)
+        out_mm(3, 1, "s")
         out_second(6, 0)
-        out_copy(4, 0, V)
+        out_second(4, 0)
+        out_copy(4, 0, S)
+        out_mm(2, 1, "t")
+        out_second(5, 0)
+        out_mm(6, 1, "t")
+        out_copy(2, 1, S)
         out_copy(5, 0, S)
+        conv(0, 1, V)
+        conv(1, 1, V)
+        out_copy(3, 1, V)
+        plane_turn(1, 0, "t")
+        plane_copy(1, 0, S)
+        conv(3, 1, V)
+        conv(2, 1, V)
         out_copy(6, 0, V)
+        plane_turn(1, 1, "t")
+        out_mm(7, 0, "v")
+        out_copy(7, 0, S)
+        out_mm(5, 1, "v")
+        plane_copy(1, 1, V)
         plane_quant(1, 0)
-        tags = ["v", "v", "v", "t", "s", "t", "s", "t"]
-        seq = [("o", 7, 0)] + [("T", 0, j) for j in range(4, 8)]
-        seq += [("o", i, 1) for i in range(4, 8)] + [("T", 1, j) for j in range(4, 8)]
-        for n, (kind, a, b) in enumerate(seq):
-            eng = S if n % 2 == 0 else V
-            if kind == "o":
-                out_mm(a, b, tags[n % 8])
-                out_copy(a, b, eng)
-            else:
-                outT_mm(a, b, tags[n % 8])
-                outT_copy(a, b, eng)
-                if b % 4 == 3:
-                    plane_quant(a, b // 4)
+        out_mm(7, 1, "s")
+        conv(4, 0, V)
+        out_mm(4, 1, "v")
+        conv(5, 0, V)
+        plane_turn(0, 2, "t")
+        conv(6, 0, V)
+        out_copy(6, 1, S)
+        out_copy(5, 1, S)
+        conv(7, 0, V)
+        out_copy(4, 1, S)
+        out_copy(7, 1, V)
+        plane_turn(0, 3, "s")
+        plane_copy(0, 2, S)
+        conv(4, 1, V)
+        conv(7, 1, V)
+        conv(5, 1, V)
+        plane_turn(1, 2, "t")
+        plane_copy(0, 3, S)
+        plane_quant(0, 1)
+        plane_copy(1, 2, S)
+        conv(6, 1, V)
+        plane_turn(1, 3, "v")
+        plane_copy(1, 3, S)
+        plane_quant(1, 1)

@@ -20,6 +20,7 @@ ACT = mybir.ActivationFunctionType
 V = 0
 S = 1
 M0_PIECES = 1
+BANKS = {"t": 3, "s": 2, "v": 3}
 TINY = 2.0**-100
 
 
@@ -45,6 +46,7 @@ def tile_differencesumouterproduct_kernel(tc, g, wg_words, wg_scales, x, q, m0, 
         lo = keep.tile([128, 8], F32, name="lo")
         rho = keep.tile([128, 8], F32, name="rho")
         warm = keep.tile([128, 1], F32, name="warm")
+        wt = keep.tile([128, 512], BF16, name="wt", align_bytes=64)
         act_codes = {}
         act_scales = {}
         for mat in ("g", "q"):
@@ -63,6 +65,7 @@ def tile_differencesumouterproduct_kernel(tc, g, wg_words, wg_scales, x, q, m0, 
                 out=rt[:].rearrange("p (a t) -> p a t", a=2),
                 in_=vec.rearrange("(a p t) -> p a t", a=2, t=4),
             )
+        nc.vector.memset(wt[:], 0.0)
         nc.vector.memset(warm[:], 0.0)
         nc.gpsimd.memset(wgs[:].rearrange("p g n -> p (g n)").bitcast(I32), 0)
         make_identity(nc, ident[:])
@@ -107,9 +110,9 @@ def tile_differencesumouterproduct_kernel(tc, g, wg_words, wg_scales, x, q, m0, 
                 out=wgs[32 * Q : 32 * Q + 4].bitcast(I32),
                 in_=wg_scales[:, 4 * Q : 4 * Q + 4, :].rearrange("g r n -> r g n").bitcast(I32),
             )
-        load_m0(0)
         load_act("q", 0, 4)
         load_act("g", 0, 4)
+        load_m0(0)
         load_wg(0)
         load_x(0, 0)
         load_act("g", 1)
@@ -121,7 +124,12 @@ def tile_differencesumouterproduct_kernel(tc, g, wg_words, wg_scales, x, q, m0, 
         load_x(1, 1)
 
         def bank(tag):
-            return psum.tile([128, 512], F32, name="bank_" + tag, tag=tag, bufs={"t": 3, "s": 2, "v": 3}[tag])
+            return psum.tile([128, 512], F32, name="bank_" + tag, tag=tag, bufs=BANKS[tag])
+
+        def warm_mm(count, tag):
+            for r in range(count):
+                b = bank(tag)
+                nc.tensor.matmul(b[:], lhsT=wt[:, :128], rhs=wt[:], start=True, stop=True)
 
         il = {}
 
@@ -442,260 +450,270 @@ def tile_differencesumouterproduct_kernel(tc, g, wg_words, wg_scales, x, q, m0, 
                     in_=pl_scales[gb][32 * Q : 32 * Q + 4, ah * 512 : (ah + 1) * 512].bitcast(I32),
                 )
 
-        m0_il(0, 1, V)
-        m0_quant(0, 1)
         prep()
-        m0_il(0, 0, S)
+        warm_mm(8, "v")
         turn_mm("q", 0, 0)
-        turn_copy("q", 0, 0, S)
         turn_mm("q", 0, 1)
         turn_copy("q", 0, 1, S)
-        turn_mm("q", 0, 3)
-        turn_copy("q", 0, 3, S)
-        turn_mm("g", 0, 0)
-        m0_quant(0, 0)
+        turn_copy("q", 0, 0, S)
+        act_quant("q", 0, 0)
         turn_mm("q", 0, 2)
         turn_copy("q", 0, 2, V)
-        turn_copy("g", 0, 0, S)
+        warm_mm(1, "v")
+        warm_mm(1, "v")
+        turn_mm("q", 0, 3)
+        turn_copy("q", 0, 3, V)
         turn_mm("g", 0, 1)
-        turn_copy("g", 0, 1, S)
-        act_quant("q", 0, 0)
-        turn_mm("g", 0, 2)
-        turn_copy("g", 0, 2, S)
+        turn_mm("g", 0, 0)
+        turn_copy("g", 0, 0, S)
         act_quant("q", 0, 1)
+        turn_copy("g", 0, 1, V)
         act_quant("g", 0, 0)
+        turn_mm("g", 0, 2)
+        turn_copy("g", 0, 2, V)
         turn_mm("g", 0, 3)
-        turn_copy("g", 0, 3, V)
+        warm_mm(1, "v")
+        m0_il(0, 1, V)
+        mm_gt(0, 1)
+        m0_il(0, 0, S)
+        m0_quant(0, 0)
+        mm_gt(0, 0)
+        m0_quant(0, 1)
+        warm_mm(1, "v")
         mm_ph(0, 0)
-        act_quant("g", 0, 1)
         tanh(0, 0)
+        y(0, 1)
+        clamp(0, 1)
         mm_ph(0, 1)
         tanh(0, 1)
-        scale(0, "ph", "ph", 1)
-        mm_gt(0, 0)
-        y(0, 0)
+        turn_copy("g", 0, 3, V)
+        act_quant("g", 0, 1)
         mm_ph(0, 2)
         scale(0, "ph", "ph", 0)
-        clamp(0, 0)
-        mm_gt(0, 1)
         mm_ph(0, 3)
-        y(0, 1)
         mm_gt(0, 2)
-        y(0, 2)
-        mm_gt(0, 3)
         tanh(0, 2)
+        y(0, 0)
+        clamp(0, 0)
+        scale(0, "ph", "ph", 1)
         scale(0, "ph", "ph", 2)
-        turn_mm("g", 1, 0)
+        mm_gt(0, 3)
+        y(0, 2)
         tanh(0, 3)
+        warm_mm(1, "v")
         scale(0, "ph", "ph", 3)
-        turn_mm("g", 1, 1)
-        turn_mm("g", 1, 2)
-        turn_mm("g", 1, 3)
+        turn_mm("g", 1, 0)
         turn_copy("g", 1, 0, S)
+        turn_mm("g", 1, 1)
         y(0, 3)
-        clamp(0, 2)
-        clamp(0, 3)
-        clamp(0, 1)
-        turn_mm("q", 1, 0)
-        e_sum(0)
         turn_copy("g", 1, 1, S)
-        turn_copy("g", 1, 2, S)
+        turn_mm("g", 1, 3)
+        turn_mm("g", 1, 2)
         turn_copy("g", 1, 3, S)
-        turn_copy("q", 1, 0, S)
+        warm_mm(1, "v")
+        warm_mm(1, "v")
+        clamp(0, 2)
+        turn_copy("g", 1, 2, S)
         turn_mm("q", 1, 1)
-        m0_il(1, 1, S)
-        turn_mm("q", 1, 3)
-        turn_copy("q", 1, 3, S)
+        clamp(0, 3)
+        e_sum(0)
+        turn_mm("q", 1, 0)
         act_quant("g", 1, 0)
         mm_gt(1, 1)
-        turn_mm("q", 1, 2)
+        m0_il(1, 0, S)
+        turn_copy("q", 1, 1, S)
+        turn_mm("q", 1, 3)
+        turn_copy("q", 1, 3, S)
         r_mul(0)
+        turn_copy("q", 1, 0, V)
         act_quant("g", 1, 1)
+        turn_mm("q", 1, 2)
+        act_quant("q", 1, 0)
+        y(1, 1)
+        m0_il(1, 1, S)
+        turn_copy("q", 1, 2, S)
         mm_gt(1, 0)
         y(1, 0)
         mm_gt(1, 2)
-        mm_gt(1, 3)
-        mm_gt(2, 0)
-        turn_copy("q", 1, 1, S)
-        y(1, 1)
         y(1, 2)
-        act_quant("q", 1, 0)
-        mm_ph(1, 0)
-        turn_copy("q", 1, 2, S)
-        mm_gt(2, 1)
-        clamp(1, 1)
-        m0_il(1, 0, S)
-        scale(1, "cp", "p", 1)
-        y(1, 3)
         lr_quant(0, "r")
-        clamp(1, 0)
-        tanh(1, 0)
         mm_ph(1, 1)
         act_quant("q", 1, 1)
-        mm_ph(1, 2)
-        mm_ph(1, 3)
+        clamp(1, 1)
+        mm_ph(1, 0)
+        mm_gt(1, 3)
+        y(1, 3)
         tanh(1, 1)
-        clamp(1, 2)
+        tanh(1, 0)
         scale(1, "ph", "ph", 0)
-        scale(1, "ph", "ph", 1)
-        mm_gt(2, 2)
-        scale(1, "cp", "p", 0)
-        tanh(1, 2)
         l_diff(0)
-        tanh(1, 3)
-        scale(1, "cph", "ph", 1)
-        scale(1, "ph", "ph", 3)
-        scale(1, "ph", "ph", 2)
+        scale(1, "cp", "p", 1)
         clamp(1, 3)
-        scale(1, "cp", "p", 3)
-        scale(1, "cph", "ph", 0)
-        mm_gt(2, 3)
-        m0_quant(1, 1)
+        mm_gt(2, 2)
+        lr_quant(0, "l")
+        y(2, 2)
+        clamp(1, 0)
+        scale(1, "ph", "ph", 1)
+        mm_ph(1, 3)
         m0_quant(1, 0)
-        mm_ph(2, 1)
-        tanh(2, 1)
+        tanh(1, 3)
+        mm_gt(2, 0)
+        mm_gt(2, 3)
+        scale(1, "cph", "ph", 1)
+        mm_ph(1, 2)
+        tanh(1, 2)
+        scale(1, "cph", "ph", 0)
+        mm_gt(2, 1)
+        scale(1, "cp", "p", 3)
         y(2, 0)
-        scale(1, "cph", "ph", 2)
+        mm_gt(3, 0)
+        scale(1, "ph", "ph", 2)
+        scale(1, "ph", "ph", 3)
         scale(1, "cph", "ph", 3)
+        scale(1, "cp", "p", 0)
+        scale(1, "cph", "ph", 2)
+        clamp(1, 2)
+        m0_quant(1, 1)
         mm_ph(2, 0)
         tanh(2, 0)
-        y(2, 2)
-        lr_quant(0, "l")
-        clamp(2, 0)
+        l_diff(1)
+        y(2, 3)
         scale(1, "cp", "p", 2)
-        mm_gt(3, 2)
+        scale(2, "ph", "ph", 0)
+        mm_ph(2, 1)
+        tanh(2, 1)
+        r_join(1)
+        scale(2, "ph", "ph", 1)
         mm_ph(2, 2)
         tanh(2, 2)
+        scale(2, "ph", "ph", 2)
+        clamp(2, 2)
         mm_ph(2, 3)
         tanh(2, 3)
-        y(2, 1)
-        scale(2, "ph", "ph", 0)
-        l_diff(1)
         mm_ph(3, 0)
-        y(2, 3)
-        r_join(1)
-        scale(2, "ph", "ph", 3)
-        scale(2, "ph", "ph", 2)
-        mm_ph(3, 1)
-        mm_gt(3, 0)
-        mm_ph(3, 2)
-        scale(2, "ph", "ph", 1)
         tanh(3, 0)
+        scale(2, "cp", "p", 2)
+        scale(2, "ph", "ph", 3)
+        y(2, 1)
+        clamp(2, 0)
+        scale(2, "cp", "p", 0)
+        mm_ph(3, 1)
+        mm_ph(3, 3)
+        lr_quant(1, "l")
+        mm_gt(3, 2)
+        lr_quant(1, "r")
+        out_mm(2, 0, "t")
+        mm_gt(3, 1)
+        scale(2, "cph", "ph", 1)
+        scale(2, "cph", "ph", 3)
+        scale(2, "cph", "ph", 2)
         clamp(2, 3)
+        scale(2, "cp", "p", 3)
         clamp(2, 1)
         scale(2, "cp", "p", 1)
-        scale(2, "cph", "ph", 2)
-        lr_quant(1, "r")
-        tanh(3, 2)
-        clamp(2, 2)
-        lr_quant(1, "l")
         scale(2, "cph", "ph", 0)
-        scale(2, "cp", "p", 0)
-        y(3, 0)
-        scale(2, "cph", "ph", 3)
-        out_mm(0, 0, "t")
-        out_copy(0, 0, V)
-        y(3, 2)
-        scale(2, "cp", "p", 3)
-        out_mm(1, 0, "t")
-        out_mm(2, 0, "t")
-        out_copy(2, 0, V)
-        scale(2, "cp", "p", 2)
-        out_copy(1, 0, S)
-        scale(2, "cph", "ph", 1)
-        mm_gt(3, 1)
-        y(3, 1)
-        tanh(3, 1)
-        outT_mm(0, 0, "t")
-        outT_copy(0, 0, V)
-        scale(3, "ph", "ph", 2)
-        mm_gt(3, 3)
-        scale(3, "ph", "ph", 0)
-        y(3, 3)
-        scale(3, "ph", "ph", 1)
-        mm_ph(3, 3)
         tanh(3, 3)
-        outT_mm(0, 3, "s")
-        scale(3, "cph", "ph", 2)
-        clamp(3, 2)
-        clamp(3, 1)
-        clamp(3, 3)
-        scale(3, "cp", "p", 3)
-        r_join(2)
+        y(3, 0)
+        out_copy(2, 0, V)
+        y(3, 2)
+        y(3, 1)
+        out_mm(1, 0, "t")
         clamp(3, 0)
-        scale(3, "ph", "ph", 3)
+        mm_gt(3, 3)
+        out_mm(0, 0, "t")
+        y(3, 3)
         outT_mm(0, 1, "t")
-        l_diff(2)
-        lr_quant(2, "l")
-        scale(3, "cph", "ph", 0)
-        scale(3, "cph", "ph", 3)
-        scale(3, "cp", "p", 0)
-        scale(3, "cp", "p", 2)
-        scale(3, "cp", "p", 1)
-        out_first(4, 0, "v")
-        out_first(5, 0, "v")
-        scale(3, "cph", "ph", 1)
-        lr_quant(2, "r")
+        clamp(3, 1)
+        r_join(2)
+        tanh(3, 1)
+        scale(3, "ph", "ph", 3)
+        mm_ph(3, 2)
+        out_copy(1, 0, S)
+        tanh(3, 2)
+        scale(3, "ph", "ph", 2)
+        outT_mm(0, 3, "s")
+        out_copy(0, 0, S)
         out_mm(3, 0, "t")
+        scale(3, "cph", "ph", 3)
+        outT_mm(0, 0, "t")
+        l_diff(2)
+        clamp(3, 2)
+        scale(3, "ph", "ph", 1)
+        lr_quant(2, "l")
+        out_first(5, 0, "v")
+        out_first(6, 0, "v")
+        scale(3, "ph", "ph", 0)
+        scale(3, "cp", "p", 1)
+        scale(3, "cph", "ph", 1)
+        scale(3, "cph", "ph", 2)
+        clamp(3, 3)
+        l_diff(3, 0, 256)
+        l_diff(3, 256, 512)
+        lr_quant(2, "r")
+        scale(3, "cph", "ph", 0)
+        scale(3, "cp", "p", 2)
+        scale(3, "cp", "p", 0)
+        scale(3, "cp", "p", 3)
         out_copy(3, 0, S)
+        outT_copy(0, 3, S)
+        out_first(4, 0, "v")
+        lr_quant(3, "l", 0, 256)
+        out_second(4, 0)
         outT_mm(0, 2, "s")
+        outT_copy(0, 1, S)
+        out_copy(4, 0, S)
+        out_second(5, 0)
+        out_copy(5, 0, S)
         outT_copy(0, 2, S)
-        l_diff(3)
         r_join(3)
         lr_quant(3, "r")
-        outT_copy(0, 1, S)
-        out_first(6, 0, "v")
-        outT_copy(0, 3, S)
-        plane_quant(0, 0)
-        lr_quant(3, "l")
-        out_mm(0, 1, "t")
-        out_copy(0, 1, S)
-        out_mm(1, 1, "s")
-        out_copy(1, 1, V)
         out_mm(3, 1, "s")
-        out_second(6, 0)
-        out_second(4, 0)
-        out_copy(4, 0, S)
+        out_copy(3, 1, S)
+        out_mm(0, 1, "t")
+        out_mm(1, 1, "s")
         out_mm(2, 1, "t")
-        out_second(5, 0)
-        out_mm(6, 1, "t")
-        out_copy(2, 1, S)
-        out_copy(5, 0, S)
-        conv(0, 1, V)
-        conv(1, 1, V)
-        out_copy(3, 1, V)
-        plane_turn(1, 0, "t")
-        plane_copy(1, 0, S)
-        conv(3, 1, V)
-        conv(2, 1, V)
-        out_copy(6, 0, V)
-        plane_turn(1, 1, "t")
-        out_mm(7, 0, "v")
-        out_copy(7, 0, S)
-        out_mm(5, 1, "v")
-        plane_copy(1, 1, V)
-        plane_quant(1, 0)
+        lr_quant(3, "l", 256, 512)
+        out_second(6, 0)
         out_mm(7, 1, "s")
-        conv(4, 0, V)
+        out_copy(0, 1, S)
+        outT_copy(0, 0, V)
+        plane_quant(0, 0)
+        out_mm(6, 1, "t")
+        out_copy(6, 0, S)
+        out_mm(7, 0, "v")
+        conv(0, 1, V)
+        out_copy(1, 1, V)
+        out_copy(2, 1, V)
+        conv(2, 1, V)
         out_mm(4, 1, "v")
+        conv(1, 1, V)
+        out_copy(7, 0, V)
+        conv(4, 0, V)
+        plane_turn(1, 0, "t")
+        conv(3, 1, V)
+        plane_turn(1, 1, "t")
+        outT_mm(1, 4, "t")
+        out_copy(6, 1, S)
+        plane_copy(1, 0, S)
+        out_copy(4, 1, V)
         conv(5, 0, V)
         plane_turn(0, 2, "t")
         conv(6, 0, V)
-        out_copy(6, 1, S)
-        out_copy(5, 1, S)
+        plane_copy(1, 1, S)
+        plane_quant(1, 0)
         conv(7, 0, V)
-        out_copy(4, 1, S)
+        out_mm(5, 1, "v")
+        out_copy(5, 1, S)
         out_copy(7, 1, V)
+        plane_copy(0, 2, V)
         plane_turn(0, 3, "s")
-        plane_copy(0, 2, S)
-        conv(4, 1, V)
-        conv(7, 1, V)
-        conv(5, 1, V)
-        plane_turn(1, 2, "t")
-        plane_copy(0, 3, S)
+        plane_copy(0, 3, V)
         plane_quant(0, 1)
-        plane_copy(1, 2, S)
-        conv(6, 1, V)
-        plane_turn(1, 3, "v")
-        plane_copy(1, 3, S)
+        outT_copy(1, 4, V)
+        outT_mm(1, 7, "v")
+        outT_mm(1, 5, "v")
+        outT_copy(1, 5, S)
+        outT_mm(1, 6, "v")
+        outT_copy(1, 6, V)
+        outT_copy(1, 7, V)
         plane_quant(1, 1)

@@ -20,7 +20,7 @@ ACT = mybir.ActivationFunctionType
 V = 0
 S = 1
 M0_PIECES = 1
-BANKS = {"t": 3, "s": 2, "v": 3}
+BANKS = {"t": 2, "s": 3, "v": 3}
 TINY = 2.0**-100
 
 
@@ -450,270 +450,214 @@ def tile_differencesumouterproduct_kernel(tc, g, wg_words, wg_scales, x, q, m0, 
                     in_=pl_scales[gb][32 * Q : 32 * Q + 4, ah * 512 : (ah + 1) * 512].bitcast(I32),
                 )
 
+        def turn_mms(mat, tg, a, b):
+            for ts in range(a, b):
+                turn_mm(mat, tg, ts)
+
+        def turn_copies(mat, tg, a, b, eng):
+            for ts in range(a, b):
+                turn_copy(mat, tg, ts, eng)
+
+        def gts(k, a, b):
+            for ts in range(a, b):
+                mm_gt(k, ts)
+
+        def phs(k, a, b):
+            for ts in range(a, b):
+                mm_ph(k, ts)
+
+        def gate(k, a, b, eng):
+            for ts in range(a, b):
+                y(k, ts)
+                if eng == G:
+                    clamp(k, ts, G)
+            if eng != G:
+                for ts in range(a, b):
+                    clamp(k, ts, eng)
+
+        def tanhs(k, a, b):
+            for ts in range(a, b):
+                tanh(k, ts)
+
+        def scales(k, key, src, a, b):
+            for ts in range(a, b):
+                scale(k, key, src, ts)
+
+        turn_mms("q", 0, 0, 2)
         prep()
-        warm_mm(8, "v")
-        turn_mm("q", 0, 0)
-        turn_mm("q", 0, 1)
-        turn_copy("q", 0, 1, S)
-        turn_copy("q", 0, 0, S)
-        act_quant("q", 0, 0)
-        turn_mm("q", 0, 2)
-        turn_copy("q", 0, 2, V)
-        warm_mm(1, "v")
-        warm_mm(1, "v")
-        turn_mm("q", 0, 3)
-        turn_copy("q", 0, 3, V)
-        turn_mm("g", 0, 1)
-        turn_mm("g", 0, 0)
-        turn_copy("g", 0, 0, S)
+        turn_copies("q", 0, 1, 2, V)
+        turn_mms("q", 0, 2, 4)
+        turn_copies("q", 0, 2, 3, V)
+        turn_copies("q", 0, 0, 1, S)
+        turn_mms("g", 0, 0, 2)
+        turn_copies("q", 0, 3, 4, V)
         act_quant("q", 0, 1)
-        turn_copy("g", 0, 1, V)
-        act_quant("g", 0, 0)
-        turn_mm("g", 0, 2)
-        turn_copy("g", 0, 2, V)
-        turn_mm("g", 0, 3)
-        warm_mm(1, "v")
-        m0_il(0, 1, V)
-        mm_gt(0, 1)
+        turn_copies("g", 0, 0, 1, S)
         m0_il(0, 0, S)
+        act_quant("q", 0, 0)
+        turn_copies("g", 0, 1, 2, V)
+        act_quant("g", 0, 0)
+        m0_il(0, 1, V)
+        turn_mms("g", 0, 2, 4)
         m0_quant(0, 0)
-        mm_gt(0, 0)
         m0_quant(0, 1)
-        warm_mm(1, "v")
-        mm_ph(0, 0)
-        tanh(0, 0)
-        y(0, 1)
-        clamp(0, 1)
-        mm_ph(0, 1)
-        tanh(0, 1)
-        turn_copy("g", 0, 3, V)
+        gts(0, 0, 2)
+        turn_copies("g", 0, 3, 4, S)
+        turn_copies("g", 0, 2, 3, S)
         act_quant("g", 0, 1)
-        mm_ph(0, 2)
-        scale(0, "ph", "ph", 0)
-        mm_ph(0, 3)
-        mm_gt(0, 2)
-        tanh(0, 2)
-        y(0, 0)
-        clamp(0, 0)
-        scale(0, "ph", "ph", 1)
-        scale(0, "ph", "ph", 2)
-        mm_gt(0, 3)
-        y(0, 2)
-        tanh(0, 3)
-        warm_mm(1, "v")
-        scale(0, "ph", "ph", 3)
-        turn_mm("g", 1, 0)
-        turn_copy("g", 1, 0, S)
-        turn_mm("g", 1, 1)
-        y(0, 3)
-        turn_copy("g", 1, 1, S)
-        turn_mm("g", 1, 3)
-        turn_mm("g", 1, 2)
-        turn_copy("g", 1, 3, S)
-        warm_mm(1, "v")
-        warm_mm(1, "v")
-        clamp(0, 2)
-        turn_copy("g", 1, 2, S)
-        turn_mm("q", 1, 1)
-        clamp(0, 3)
-        e_sum(0)
-        turn_mm("q", 1, 0)
+        phs(0, 0, 2)
+        tanhs(0, 0, 2)
+        phs(0, 2, 4)
+        tanhs(0, 2, 4)
+        gate(0, 0, 2, G)
+        scales(0, "ph", "ph", 2, 4)
+        scales(0, "ph", "ph", 0, 2)
+        gts(0, 2, 4)
+        gate(0, 2, 4, G)
+        turn_mms("g", 1, 0, 2)
+        turn_copies("g", 1, 0, 1, V)
+        turn_copies("g", 1, 1, 2, V)
         act_quant("g", 1, 0)
-        mm_gt(1, 1)
-        m0_il(1, 0, S)
-        turn_copy("q", 1, 1, S)
-        turn_mm("q", 1, 3)
-        turn_copy("q", 1, 3, S)
-        r_mul(0)
-        turn_copy("q", 1, 0, V)
+        e_sum(0)
+        turn_mms("g", 1, 2, 4)
+        turn_copies("g", 1, 2, 3, S)
+        turn_copies("g", 1, 3, 4, S)
         act_quant("g", 1, 1)
-        turn_mm("q", 1, 2)
+        turn_mms("q", 1, 0, 2)
+        r_mul(0)
+        gts(1, 0, 2)
+        turn_copies("q", 1, 1, 2, S)
+        turn_copies("q", 1, 0, 1, S)
         act_quant("q", 1, 0)
-        y(1, 1)
-        m0_il(1, 1, S)
-        turn_copy("q", 1, 2, S)
-        mm_gt(1, 0)
-        y(1, 0)
-        mm_gt(1, 2)
-        y(1, 2)
-        lr_quant(0, "r")
-        mm_ph(1, 1)
-        act_quant("q", 1, 1)
-        clamp(1, 1)
-        mm_ph(1, 0)
-        mm_gt(1, 3)
-        y(1, 3)
-        tanh(1, 1)
-        tanh(1, 0)
-        scale(1, "ph", "ph", 0)
+        turn_mms("q", 1, 2, 4)
+        turn_copies("q", 1, 3, 4, S)
         l_diff(0)
-        scale(1, "cp", "p", 1)
-        clamp(1, 3)
-        mm_gt(2, 2)
-        lr_quant(0, "l")
-        y(2, 2)
-        clamp(1, 0)
-        scale(1, "ph", "ph", 1)
-        mm_ph(1, 3)
+        phs(1, 0, 2)
+        gate(1, 0, 2, G)
+        gts(1, 2, 4)
+        gate(1, 2, 4, G)
+        gts(2, 0, 2)
+        turn_copies("q", 1, 2, 3, S)
+        gate(2, 0, 2, G)
+        act_quant("q", 1, 1)
+        gts(2, 2, 4)
+        phs(1, 2, 4)
+        tanhs(1, 0, 2)
+        m0_il(1, 1, V)
+        m0_il(1, 0, S)
+        scales(1, "ph", "ph", 0, 2)
+        scales(1, "cph", "ph", 0, 2)
+        scales(1, "cp", "p", 2, 4)
+        gate(2, 2, 4, G)
         m0_quant(1, 0)
-        tanh(1, 3)
-        mm_gt(2, 0)
-        mm_gt(2, 3)
-        scale(1, "cph", "ph", 1)
-        mm_ph(1, 2)
-        tanh(1, 2)
-        scale(1, "cph", "ph", 0)
-        mm_gt(2, 1)
-        scale(1, "cp", "p", 3)
-        y(2, 0)
-        mm_gt(3, 0)
-        scale(1, "ph", "ph", 2)
-        scale(1, "ph", "ph", 3)
-        scale(1, "cph", "ph", 3)
-        scale(1, "cp", "p", 0)
-        scale(1, "cph", "ph", 2)
-        clamp(1, 2)
+        tanhs(1, 2, 4)
         m0_quant(1, 1)
-        mm_ph(2, 0)
-        tanh(2, 0)
+        scales(1, "ph", "ph", 2, 4)
+        lr_quant(0, "l")
+        gts(3, 0, 2)
+        scales(1, "cph", "ph", 2, 4)
+        scales(1, "cp", "p", 0, 2)
+        phs(2, 0, 2)
+        lr_quant(0, "r")
         l_diff(1)
-        y(2, 3)
-        scale(1, "cp", "p", 2)
-        scale(2, "ph", "ph", 0)
-        mm_ph(2, 1)
-        tanh(2, 1)
+        tanhs(2, 0, 2)
+        scales(2, "ph", "ph", 0, 2)
         r_join(1)
-        scale(2, "ph", "ph", 1)
-        mm_ph(2, 2)
-        tanh(2, 2)
-        scale(2, "ph", "ph", 2)
-        clamp(2, 2)
-        mm_ph(2, 3)
-        tanh(2, 3)
-        mm_ph(3, 0)
-        tanh(3, 0)
-        scale(2, "cp", "p", 2)
-        scale(2, "ph", "ph", 3)
-        y(2, 1)
-        clamp(2, 0)
-        scale(2, "cp", "p", 0)
-        mm_ph(3, 1)
-        mm_ph(3, 3)
         lr_quant(1, "l")
-        mm_gt(3, 2)
+        phs(2, 2, 4)
+        tanhs(2, 2, 4)
+        scales(2, "ph", "ph", 2, 4)
+        gate(3, 0, 2, G)
         lr_quant(1, "r")
-        out_mm(2, 0, "t")
-        mm_gt(3, 1)
-        scale(2, "cph", "ph", 1)
-        scale(2, "cph", "ph", 3)
-        scale(2, "cph", "ph", 2)
-        clamp(2, 3)
-        scale(2, "cp", "p", 3)
-        clamp(2, 1)
-        scale(2, "cp", "p", 1)
-        scale(2, "cph", "ph", 0)
-        tanh(3, 3)
-        y(3, 0)
-        out_copy(2, 0, V)
-        y(3, 2)
-        y(3, 1)
+        phs(3, 0, 2)
+        tanhs(3, 0, 2)
+        gts(3, 2, 4)
+        gate(3, 2, 4, G)
         out_mm(1, 0, "t")
-        clamp(3, 0)
-        mm_gt(3, 3)
-        out_mm(0, 0, "t")
-        y(3, 3)
-        outT_mm(0, 1, "t")
-        clamp(3, 1)
-        r_join(2)
-        tanh(3, 1)
-        scale(3, "ph", "ph", 3)
-        mm_ph(3, 2)
-        out_copy(1, 0, S)
-        tanh(3, 2)
-        scale(3, "ph", "ph", 2)
-        outT_mm(0, 3, "s")
-        out_copy(0, 0, S)
-        out_mm(3, 0, "t")
-        scale(3, "cph", "ph", 3)
-        outT_mm(0, 0, "t")
+        out_mm(2, 0, "t")
+        phs(3, 2, 4)
         l_diff(2)
-        clamp(3, 2)
-        scale(3, "ph", "ph", 1)
-        lr_quant(2, "l")
-        out_first(5, 0, "v")
-        out_first(6, 0, "v")
-        scale(3, "ph", "ph", 0)
-        scale(3, "cp", "p", 1)
-        scale(3, "cph", "ph", 1)
-        scale(3, "cph", "ph", 2)
-        clamp(3, 3)
-        l_diff(3, 0, 256)
-        l_diff(3, 256, 512)
-        lr_quant(2, "r")
-        scale(3, "cph", "ph", 0)
-        scale(3, "cp", "p", 2)
-        scale(3, "cp", "p", 0)
-        scale(3, "cp", "p", 3)
-        out_copy(3, 0, S)
-        outT_copy(0, 3, S)
-        out_first(4, 0, "v")
-        lr_quant(3, "l", 0, 256)
-        out_second(4, 0)
+        e_sum(2)
+        scales(3, "ph", "ph", 0, 2)
+        scales(3, "cp", "p", 0, 2)
+        tanhs(3, 2, 4)
+        scales(3, "ph", "ph", 2, 4)
+        out_copy(2, 0, S)
+        scales(3, "cph", "ph", 0, 2)
+        out_copy(1, 0, V)
         outT_mm(0, 2, "s")
-        outT_copy(0, 1, S)
-        out_copy(4, 0, S)
-        out_second(5, 0)
-        out_copy(5, 0, S)
         outT_copy(0, 2, S)
+        r_mul(2)
+        lr_quant(2, "r")
+        out_mm(0, 0, "t")
+        scales(3, "cph", "ph", 2, 4)
+        out_copy(0, 0, S)
+        scales(3, "cp", "p", 2, 4)
+        outT_mm(0, 3, "s")
+        outT_copy(0, 3, S)
+        lr_quant(2, "l")
+        outT_mm(0, 1, "t")
+        outT_mm(0, 0, "t")
+        outT_copy(0, 0, S)
+        outT_copy(0, 1, S)
         r_join(3)
+        out_first(6, 0, "v")
+        out_first(5, 0, "v")
         lr_quant(3, "r")
+        out_mm(3, 0, "t")
+        out_copy(3, 0, S)
+        out_mm(0, 1, "t")
+        out_copy(0, 1, S)
+        out_mm(1, 1, "s")
+        out_first(4, 0, "v")
+        l_diff(3)
+        out_mm(2, 1, "t")
+        out_copy(1, 1, S)
+        lr_quant(3, "l")
+        out_copy(2, 1, S)
+        plane_quant(0, 0)
+        outT_mm(1, 2, "s")
+        outT_copy(1, 2, V)
+        outT_mm(1, 1, "t")
+        out_second(6, 0)
+        out_second(5, 0)
+        out_second(4, 0)
+        out_copy(5, 0, V)
+        out_copy(6, 0, S)
+        outT_copy(1, 1, S)
+        outT_mm(1, 3, "t")
+        out_mm(7, 0, "v")
+        conv(5, 0, V)
+        out_copy(7, 0, S)
+        out_mm(5, 1, "v")
+        out_copy(4, 0, V)
+        out_copy(5, 1, S)
+        outT_copy(1, 3, V)
+        outT_mm(1, 0, "t")
+        outT_copy(1, 0, S)
+        conv(4, 0, V)
+        conv(7, 0, S)
+        conv(6, 0, V)
+        plane_quant(1, 0)
+        out_mm(7, 1, "s")
+        out_copy(7, 1, S)
+        out_mm(4, 1, "v")
+        out_copy(4, 1, V)
+        out_mm(6, 1, "t")
+        out_copy(6, 1, V)
+        plane_turn(0, 2, "t")
+        plane_turn(0, 3, "s")
+        plane_copy(0, 3, S)
+        plane_copy(0, 2, V)
+        outT_mm(1, 5, "v")
+        plane_quant(0, 1)
+        outT_mm(1, 4, "t")
+        outT_copy(1, 4, V)
         out_mm(3, 1, "s")
         out_copy(3, 1, S)
-        out_mm(0, 1, "t")
-        out_mm(1, 1, "s")
-        out_mm(2, 1, "t")
-        lr_quant(3, "l", 256, 512)
-        out_second(6, 0)
-        out_mm(7, 1, "s")
-        out_copy(0, 1, S)
-        outT_copy(0, 0, V)
-        plane_quant(0, 0)
-        out_mm(6, 1, "t")
-        out_copy(6, 0, S)
-        out_mm(7, 0, "v")
-        conv(0, 1, V)
-        out_copy(1, 1, V)
-        out_copy(2, 1, V)
-        conv(2, 1, V)
-        out_mm(4, 1, "v")
-        conv(1, 1, V)
-        out_copy(7, 0, V)
-        conv(4, 0, V)
-        plane_turn(1, 0, "t")
-        conv(3, 1, V)
-        plane_turn(1, 1, "t")
-        outT_mm(1, 4, "t")
-        out_copy(6, 1, S)
-        plane_copy(1, 0, S)
-        out_copy(4, 1, V)
-        conv(5, 0, V)
-        plane_turn(0, 2, "t")
-        conv(6, 0, V)
-        plane_copy(1, 1, S)
-        plane_quant(1, 0)
-        conv(7, 0, V)
-        out_mm(5, 1, "v")
-        out_copy(5, 1, S)
-        out_copy(7, 1, V)
-        plane_copy(0, 2, V)
-        plane_turn(0, 3, "s")
-        plane_copy(0, 3, V)
-        plane_quant(0, 1)
-        outT_copy(1, 4, V)
         outT_mm(1, 7, "v")
-        outT_mm(1, 5, "v")
-        outT_copy(1, 5, S)
+        outT_copy(1, 7, S)
         outT_mm(1, 6, "v")
-        outT_copy(1, 6, V)
-        outT_copy(1, 7, V)
+        outT_copy(1, 6, S)
+        outT_copy(1, 5, V)
         plane_quant(1, 1)

@@ -4,7 +4,11 @@ import concourse.mybir as mybir
 from concourse.masks import make_identity
 
 N = 1024
+HALF = 512
+P = 128
+SLOTS = 4
 HEBB = 0.03125
+TINY = 2.0**-100
 FLOPS = 3 * 2 * N * N * N
 
 F32 = mybir.dt.float32
@@ -17,106 +21,84 @@ FP4 = mybir.dt.float4_e2m1fn_x4
 ALU = mybir.AluOpType
 ACT = mybir.ActivationFunctionType
 
-V = 0
-S = 1
-M0_PIECES = 1
-BANKS = {"t": 2, "s": 3, "v": 3}
-TINY = 2.0**-100
+VECTOR, SCALAR = "vector", "scalar"
+
+BANKS = {"turn": 2, "tanh": 3, "gate": 3}
+CHUNKS = ((0, 0), (1, 0), (0, 1), (1, 1))
 
 
 def tile_differencesumouterproduct_kernel(tc, g, wg_words, wg_scales, x, q, m0, s, c, out_0, out_1, out_2):
     nc = tc.nc
     with ExitStack() as ctx:
         keep = ctx.enter_context(tc.tile_pool(name="keep", bufs=1))
-        raw = ctx.enter_context(tc.tile_pool(name="raw", bufs=1))
         work = ctx.enter_context(tc.tile_pool(name="work", bufs=1))
         psum = ctx.enter_context(tc.psum_pool(name="psum", bufs=1))
         ctx.enter_context(tc.manual_schedule())
 
-        ident = keep.tile([128, 128], F32, name="ident")
-        wgw = [keep.tile([128, 2, 1024], U8, name=f"wgw{h}", align_bytes=64) for h in range(2)]
-        wgs = keep.tile([128, 2, 1024], U8, name="wgs", align_bytes=64)
-        s_raw = keep.tile([128, 8], BF16, name="s_raw")
-        c_raw = keep.tile([128, 8], BF16, name="c_raw")
-        s_sb = keep.tile([128, 8], F32, name="s_sb")
-        c_sb = keep.tile([128, 8], F32, name="c_sb")
-        is0 = keep.tile([128, 8], F32, name="is0")
-        neg = keep.tile([128, 8], F32, name="neg")
-        hi = keep.tile([128, 8], F32, name="hi")
-        lo = keep.tile([128, 8], F32, name="lo")
-        rho = keep.tile([128, 8], F32, name="rho")
-        warm = keep.tile([128, 1], F32, name="warm")
-        wt = keep.tile([128, 512], BF16, name="wt", align_bytes=64)
-        act_codes = {}
-        act_scales = {}
-        for mat in ("g", "q"):
-            for tg in range(2):
-                act_codes[mat, tg] = keep.tile([128, 4, 2, 128], U32, name=f"{mat}{tg}_codes", align_bytes=64)
-                act_scales[mat, tg] = keep.tile([128, 4, 2, 128], U8, name=f"{mat}{tg}_scales", align_bytes=64)
-        m_codes = keep.tile([128, 2, N], U32, name="m_codes", align_bytes=64)
-        m_scales = keep.tile([128, 2, N], U8, name="m_scales", align_bytes=64)
-        l_codes = keep.tile([128, 2, N], U32, name="l_codes", align_bytes=64)
-        l_scales = keep.tile([128, 2, N], U8, name="l_scales", align_bytes=64)
-        r_codes = keep.tile([128, 2, N], U32, name="r_codes", align_bytes=64)
-        r_scales = keep.tile([128, 2, N], U8, name="r_scales", align_bytes=64)
+        def codes_and_scales(shape, name):
+            codes = keep.tile([P] + shape, U32, name=name + "_codes", align_bytes=64)
+            scales = keep.tile([P] + shape, U8, name=name + "_scales", align_bytes=64)
+            return codes, scales
 
-        for vec, rt in ((s, s_raw), (c, c_raw)):
+        ident = keep.tile([P, P], F32, name="ident")
+        wg_sb = [keep.tile([P, 2, 2 * HALF], U8, name=f"wg{h}", align_bytes=64) for h in range(2)]
+        wg_sc = keep.tile([P, 2, N], U8, name="wg_sc", align_bytes=64)
+        acts = {(mat, blk): codes_and_scales([SLOTS, 2, P], f"{mat}{blk}") for mat in ("g", "q") for blk in range(2)}
+        m0_mx = codes_and_scales([2, N], "m0")
+        lr_mx = {which: codes_and_scales([2, N], which) for which in ("l", "r")}
+        plane_scales = [keep.tile([P, N], U8, name=f"plane_scales{G}", align_bytes=64) for G in range(2)]
+
+        factors = {}
+        for name, vec in (("s", s), ("c", c)):
+            factors[name] = keep.tile([P, 2 * SLOTS], BF16, name=name + "_raw")
             nc.scalar.dma_start(
-                out=rt[:].rearrange("p (a t) -> p a t", a=2),
-                in_=vec.rearrange("(a p t) -> p a t", a=2, t=4),
+                out=factors[name][:].rearrange("p (b t) -> p b t", b=2),
+                in_=vec.rearrange("(b p t) -> p b t", b=2, t=SLOTS),
             )
-        nc.vector.memset(wt[:], 0.0)
-        nc.vector.memset(warm[:], 0.0)
-        nc.gpsimd.memset(wgs[:].rearrange("p g n -> p (g n)").bitcast(I32), 0)
+        zero = keep.tile([P, 1], F32, name="zero")
+        nc.vector.memset(zero[:], 0.0)
+        nc.scalar.activation(out=zero[:], in_=zero[:], func=ACT.Tanh)
+        nc.gpsimd.memset(wg_sc[:].rearrange("p g n -> p (g n)").bitcast(I32), 0)
         make_identity(nc, ident[:])
-        nc.scalar.activation(out=warm[:], in_=warm[:], func=ACT.Tanh)
 
-        raws = {}
+        raw = {}
+
+        def load_rows(mat, src, blk, pieces):
+            raw[mat, blk] = work.tile([P, SLOTS, N], BF16, name=f"{mat}_raw{blk}", tag="raw", bufs=4)
+            rows = src.rearrange("(b m t) k -> b m t k", b=2, t=SLOTS)[blk]
+            step = SLOTS // pieces
+            for t in range(0, SLOTS, step):
+                nc.sync.dma_start(out=raw[mat, blk][:, t : t + step], in_=rows[:, t : t + step])
 
         def load_m0(h):
-            t = raw.tile([128, 2, 4, 512], BF16, name=f"m0_{h}", tag="raw8k", bufs=4)
-            raws["m", h] = t
-            src = m0.rearrange("(g p j) n -> g p j n", g=2, j=4)
-            for gk in range(2):
-                for piece in range(M0_PIECES if h == 0 and gk == 0 else 1):
-                    w = 512 // (M0_PIECES if h == 0 and gk == 0 else 1)
-                    nc.sync.dma_start(
-                        out=t[:, gk, :, piece * w : (piece + 1) * w],
-                        in_=src[gk, :, :, h * 512 + piece * w : h * 512 + (piece + 1) * w],
-                    )
+            raw["m0", h] = work.tile([P, 2, SLOTS, HALF], BF16, name=f"m0_raw{h}", tag="raw", bufs=4)
+            rows = m0.rearrange("(g p t) n -> g p t n", g=2, t=SLOTS)
+            for G in range(2):
+                nc.sync.dma_start(out=raw["m0", h][:, G], in_=rows[G, :, :, h * HALF : (h + 1) * HALF])
 
-        def load_act(mat, tg, parts=2):
-            t = raw.tile([128, 4, 1024], BF16, name=f"{mat}_{tg}", tag="raw8k", bufs=4)
-            raws[mat, tg] = t
-            src = (g if mat == "g" else q).rearrange("(tg m t) k -> tg m t k", tg=2, t=4)
-            step = 4 // parts
-            for a in range(0, 4, step):
-                nc.sync.dma_start(out=t[:, a : a + step], in_=src[tg, :, a : a + step, :])
-
-        def load_x(tg, h):
-            t = raw.tile([128, 4, 512], BF16, name=f"x_{tg}{h}", tag="x", bufs=4)
-            raws["x", tg, h] = t
-            src = x.rearrange("(tg m t) n -> tg m t n", tg=2, t=4)
-            nc.sync.dma_start(out=t[:], in_=src[tg, :, :, h * 512 : (h + 1) * 512])
+        def load_x(blk, h):
+            raw["x", blk, h] = work.tile([P, SLOTS, HALF], BF16, name=f"x_raw{blk}{h}", tag="x", bufs=3)
+            rows = x.rearrange("(b m t) n -> b m t n", b=2, t=SLOTS)[blk]
+            nc.sync.dma_start(out=raw["x", blk, h][:], in_=rows[:, :, h * HALF : (h + 1) * HALF])
 
         def load_wg(h):
             nc.sync.dma_start(
-                out=wgw[h][:].bitcast(I32),
-                in_=wg_words[:, :, h * 1024 : (h + 1) * 1024].rearrange("g p b -> p g b").bitcast(I32),
+                out=wg_sb[h][:].bitcast(I32),
+                in_=wg_words[:, :, 2 * h * HALF : 2 * (h + 1) * HALF].rearrange("g p b -> p g b").bitcast(I32),
             )
 
+        load_rows("q", q, 0, pieces=4)
+        load_rows("g", g, 0, pieces=4)
         for Q in range(4):
-            nc.gpsimd.dma_start(
-                out=wgs[32 * Q : 32 * Q + 4].bitcast(I32),
+            nc.sync.dma_start(
+                out=wg_sc[32 * Q : 32 * Q + 4].bitcast(I32),
                 in_=wg_scales[:, 4 * Q : 4 * Q + 4, :].rearrange("g r n -> r g n").bitcast(I32),
             )
-        load_act("q", 0, 4)
-        load_act("g", 0, 4)
         load_m0(0)
         load_wg(0)
         load_x(0, 0)
-        load_act("g", 1)
-        load_act("q", 1)
+        load_rows("g", g, 1, pieces=2)
+        load_rows("q", q, 1, pieces=2)
         load_x(1, 0)
         load_m0(1)
         load_wg(1)
@@ -124,540 +106,506 @@ def tile_differencesumouterproduct_kernel(tc, g, wg_words, wg_scales, x, q, m0, 
         load_x(1, 1)
 
         def bank(tag):
-            return psum.tile([128, 512], F32, name="bank_" + tag, tag=tag, bufs=BANKS[tag])
+            return psum.tile([P, HALF], F32, name="bank_" + tag, tag=tag, bufs=BANKS[tag])
 
-        def warm_mm(count, tag):
-            for r in range(count):
-                b = bank(tag)
-                nc.tensor.matmul(b[:], lhsT=wt[:, :128], rhs=wt[:], start=True, stop=True)
-
-        il = {}
-
-        G = 2
-
-        def m0_il(h, gk, eng, lo=0, hi=512):
-            if ("m", h, gk) not in il:
-                il["m", h, gk] = work.tile([128, 2048], BF16, name=f"m_il{h}{gk}", tag="il", bufs=5, align_bytes=64)
-            t = il["m", h, gk]
-            o = t[:, 4 * lo : 4 * hi].rearrange("p (c i j) -> p c j i", i=4, j=4)
-            i = raws["m", h][:, gk, :, lo:hi].rearrange("p j (c i) -> p c j i", i=4)
-            if eng == V:
-                nc.vector.tensor_copy(out=o, in_=i)
-            elif eng == G:
-                nc.gpsimd.tensor_scalar(out=o, in0=i, scalar1=1.0, scalar2=0.0, op0=ALU.mult, op1=ALU.add)
+        def copy(engine, out, in_):
+            if engine == VECTOR:
+                nc.vector.tensor_copy(out=out, in_=in_)
             else:
-                nc.scalar.copy(out=o, in_=i)
+                nc.scalar.copy(out=out, in_=in_)
 
-        def m0_quant(h, gk):
-            nc.vector.quantize_mx(
-                out=m_codes[:, gk, h * 512 : (h + 1) * 512].bitcast(FP8),
-                scales=m_scales[:, gk, h * 512 : (h + 1) * 512],
-                in_=il["m", h, gk][:],
+        def copy_times_hebb(engine, out, in_):
+            if engine == VECTOR:
+                nc.vector.tensor_scalar(out=out, in0=in_, scalar1=HEBB, scalar2=None, op0=ALU.mult)
+            else:
+                nc.scalar.activation(out=out, in_=in_, func=ACT.Copy, scale=HEBB)
+
+        def mx_pass(out, lhsT, lhsT_scale, rhs, rhs_scale, G, rhs_dtype=FP8):
+            nc.tensor.matmul_mx(
+                out=out,
+                lhsT=lhsT.bitcast(FP8),
+                lhsT_scale=lhsT_scale,
+                rhs=rhs.bitcast(rhs_dtype),
+                rhs_scale=rhs_scale,
+                start=(G == 0),
+                stop=(G == 1),
             )
 
+        def factors_ready():
+            def column_tile(name):
+                factors[name] = keep.tile([P, 2 * SLOTS], F32, name=name)
+                return factors[name][:]
+
+            s32, c32, is_zero, minus = [column_tile(name) for name in ("s32", "c32", "is_zero", "minus")]
+            ratio, high, low = [column_tile(name) for name in ("ratio", "high", "low")]
+            nc.vector.tensor_copy(out=s32, in_=factors["s"][:])
+            nc.vector.tensor_copy(out=c32, in_=factors["c"][:])
+            nc.vector.tensor_scalar(out=is_zero, in0=s32, scalar1=0.0, scalar2=TINY, op0=ALU.is_equal, op1=ALU.mult)
+            nc.vector.tensor_tensor(out=s32, in0=s32, in1=is_zero, op=ALU.add)
+            nc.vector.tensor_scalar(out=minus, in0=s32, scalar1=-1.0, scalar2=None, op0=ALU.mult)
+            nc.vector.reciprocal(out=ratio, in_=s32)
+            nc.vector.tensor_tensor(out=high, in0=s32, in1=minus, op=ALU.max)
+            nc.vector.tensor_tensor(out=ratio, in0=ratio, in1=c32, op=ALU.mult)
+            nc.vector.tensor_tensor(out=low, in0=s32, in1=minus, op=ALU.min)
+
+        def factor(name, k, t):
+            column = CHUNKS[k][0] * SLOTS + t
+            return factors[name][:, column : column + 1]
+
+        grouped = {}
         turned = {}
 
-        def turn_mm(mat, tg, ts):
-            b = bank("t")
-            turned[mat, tg, ts] = b
-            words = raws[mat, tg][:, ts, :].bitcast(F32)
-            for gk in range(2):
-                for u in range(2):
-                    k = 2 * gk + u
-                    nc.tensor.transpose(
-                        b[:, k * 128 : (k + 1) * 128], words[:, 256 * gk + u : 256 * (gk + 1) : 2], ident[:]
+        def grouped_tile(key, name):
+            if key not in grouped:
+                grouped[key] = work.tile([P, HALF * SLOTS], BF16, name=name, tag="grouped", bufs=5, align_bytes=64)
+            return grouped[key]
+
+        def transpose_rows(mat, blk, first, last):
+            for t in range(first, last):
+                turned[mat, blk, t] = bank("turn")
+                words = raw[mat, blk][:, t, :].bitcast(F32)
+                for G in range(2):
+                    for u in range(2):
+                        at = (2 * G + u) * P
+                        nc.tensor.transpose(
+                            turned[mat, blk, t][:, at : at + P], words[:, 256 * G + u : 256 * (G + 1) : 2], ident[:]
+                        )
+
+        def group_rows(mat, blk, first, last, engine):
+            for t in range(first, last):
+                tile = grouped_tile((mat, blk, t // 2), f"{mat}_grouped{blk}{t // 2}")
+                words = tile[:].bitcast(F32)[:, (t % 2) * HALF : (t % 2 + 1) * HALF]
+                copy(
+                    engine,
+                    out=words.rearrange("p (g m u) -> p g m u", g=2, u=2),
+                    in_=turned[mat, blk, t][:].rearrange("p (g u m) -> p g m u", g=2, u=2),
+                )
+
+        def quantise_rows(mat, blk, pair):
+            codes, scales = acts[mat, blk]
+            both = slice(2 * pair, 2 * pair + 2)
+            nc.vector.quantize_mx(
+                out=codes[:, both].rearrange("p t g m -> p (t g m)").bitcast(FP8),
+                scales=scales[:, both].rearrange("p t g m -> p (t g m)"),
+                in_=grouped[mat, blk, pair][:],
+            )
+
+        def group_m0(h, G, engine):
+            copy(
+                engine,
+                out=grouped_tile(("m0", h, G), f"m0_grouped{h}{G}")[:].rearrange("p (c i t) -> p c t i", i=4, t=SLOTS),
+                in_=raw["m0", h][:, G].rearrange("p t (c i) -> p c t i", i=4),
+            )
+
+        def quantise_m0(h, G):
+            codes, scales = m0_mx
+            cols = slice(h * HALF, (h + 1) * HALF)
+            nc.vector.quantize_mx(
+                out=codes[:, G, cols].bitcast(FP8), scales=scales[:, G, cols], in_=grouped["m0", h, G][:]
+            )
+
+        product = {}
+        tiles = {}
+
+        def chunk_tile(key, k, bufs):
+            if (key, k) not in tiles:
+                tiles[key, k] = work.tile([P, SLOTS, HALF], F32, name=f"{key}{k}", tag=key, bufs=bufs)
+            return tiles[key, k]
+
+        def products_gate(k, first, last):
+            blk, h = CHUNKS[k]
+            codes, scales = acts["g", blk]
+            for t in range(first, last):
+                product["gate", k, t] = bank("gate")
+                for G in range(2):
+                    mx_pass(
+                        product["gate", k, t][:],
+                        codes[:, t, G, :],
+                        scales[:, t, G, :],
+                        wg_sb[h][:, G, :],
+                        wg_sc[:, G, h * HALF : (h + 1) * HALF],
+                        G,
+                        rhs_dtype=FP4,
                     )
 
-        def turn_copy(mat, tg, ts, eng):
-            b = turned[mat, tg, ts]
-            if (mat, tg, ts // 2) not in il:
-                il[mat, tg, ts // 2] = work.tile(
-                    [128, 2048], BF16, name=f"{mat}_il{tg}{ts}", tag="il", bufs=5, align_bytes=64
+        def products_tanh(k, first, last):
+            blk, h = CHUNKS[k]
+            codes, scales = acts["q", blk]
+            for t in range(first, last):
+                product["tanh", k, t] = bank("tanh")
+                for G in range(2):
+                    mx_pass(
+                        product["tanh", k, t][:],
+                        codes[:, t, G, :],
+                        scales[:, t, G, :],
+                        m0_mx[0][:, G, h * HALF : (h + 1) * HALF],
+                        m0_mx[1][:, G, h * HALF : (h + 1) * HALF],
+                        G,
+                    )
+
+        def gate(k, first, last):
+            blk, h = CHUNKS[k]
+            sp = chunk_tile("sp", k, bufs=2)
+            for t in range(first, last):
+                nc.vector.scalar_tensor_tensor(
+                    out=sp[:, t, :],
+                    in0=product["gate", k, t][:],
+                    scalar=factor("s32", k, t),
+                    in1=raw["x", blk, h][:, t, :],
+                    op0=ALU.mult,
+                    op1=ALU.mult,
                 )
-            o = il[mat, tg, ts // 2][:].bitcast(F32)[:, (ts % 2) * 512 : (ts % 2 + 1) * 512]
-            o = o.rearrange("p (g m u) -> p g m u", g=2, u=2)
-            i = b[:].rearrange("p (g u m) -> p g m u", g=2, u=2)
-            if eng == V:
-                nc.vector.tensor_copy(out=o, in_=i)
-            else:
-                nc.scalar.copy(out=o, in_=i)
-
-        def act_quant(mat, tg, pair):
-            nc.vector.quantize_mx(
-                out=act_codes[mat, tg][:, 2 * pair : 2 * pair + 2].rearrange("p a b c -> p (a b c)").bitcast(FP8),
-                scales=act_scales[mat, tg][:, 2 * pair : 2 * pair + 2].rearrange("p a b c -> p (a b c)"),
-                in_=il[mat, tg, pair][:],
-            )
-
-        chunks = ((0, 0), (1, 0), (0, 1), (1, 1))
-        gt_bank = {}
-        ph_bank = {}
-
-        def mm_gt(k, ts):
-            tg, h = chunks[k]
-            b = bank("v")
-            gt_bank[k, ts] = b
-            for gk in range(2):
-                nc.tensor.matmul_mx(
-                    out=b[:],
-                    lhsT=act_codes["g", tg][:, ts, gk, :].bitcast(FP8),
-                    lhsT_scale=act_scales["g", tg][:, ts, gk, :],
-                    rhs=wgw[h][:, gk, :].bitcast(FP4),
-                    rhs_scale=wgs[:, gk, h * 512 : (h + 1) * 512],
-                    start=(gk == 0),
-                    stop=(gk == 1),
+                nc.gpsimd.tensor_scalar(
+                    out=sp[:, t, :],
+                    in0=sp[:, t, :],
+                    scalar1=factor("high", k, t),
+                    scalar2=factor("low", k, t),
+                    op0=ALU.min,
+                    op1=ALU.max,
                 )
 
-        def mm_ph(k, ts):
-            tg, h = chunks[k]
-            b = bank("s")
-            ph_bank[k, ts] = b
-            for gk in range(2):
-                nc.tensor.matmul_mx(
-                    out=b[:],
-                    lhsT=act_codes["q", tg][:, ts, gk, :].bitcast(FP8),
-                    lhsT_scale=act_scales["q", tg][:, ts, gk, :],
-                    rhs=m_codes[:, gk, h * 512 : (h + 1) * 512].bitcast(FP8),
-                    rhs_scale=m_scales[:, gk, h * 512 : (h + 1) * 512],
-                    start=(gk == 0),
-                    stop=(gk == 1),
+        def tanhs(k, first, last):
+            sph = chunk_tile("sph", k, bufs=2)
+            for t in range(first, last):
+                nc.scalar.activation(out=sph[:, t, :], in_=product["tanh", k, t][:], func=ACT.Tanh, bias=zero[:])
+
+        def times_s(k, first, last):
+            sph = tiles["sph", k]
+            for t in range(first, last):
+                nc.scalar.activation(out=sph[:, t, :], in_=sph[:, t, :], func=ACT.Copy, scale=factor("s32", k, t))
+
+        def times_ratio(k, src, first, last):
+            out = chunk_tile("c_from_" + src, k, bufs=1)
+            for t in range(first, last):
+                nc.scalar.activation(
+                    out=out[:, t, :], in_=tiles[src, k][:, t, :], func=ACT.Copy, scale=factor("ratio", k, t)
                 )
 
-        pt = {}
-
-        def y(k, ts):
-            tg, h = chunks[k]
-            if ("p", k) not in pt:
-                pt["p", k] = work.tile([128, 4, 512], F32, name=f"p{k}", tag="p", bufs=2)
-            nc.vector.scalar_tensor_tensor(
-                out=pt["p", k][:, ts, :],
-                in0=gt_bank[k, ts][:],
-                scalar=s_sb[:, tg * 4 + ts : tg * 4 + ts + 1],
-                in1=raws["x", tg, h][:, ts, :],
-                op0=ALU.mult,
-                op1=ALU.mult,
-            )
-
-        def clamp(k, ts, eng=V):
-            tg, h = chunks[k]
-            t = pt["p", k][:, ts]
-            col = tg * 4 + ts
-            (nc.gpsimd if eng == G else nc.vector).tensor_scalar(
-                out=t,
-                in0=t,
-                scalar1=hi[:, col : col + 1],
-                scalar2=lo[:, col : col + 1],
-                op0=ALU.min,
-                op1=ALU.max,
-            )
-
-        def prep():
-            nc.vector.tensor_copy(out=s_sb[:], in_=s_raw[:])
-            nc.vector.tensor_copy(out=c_sb[:], in_=c_raw[:])
-            nc.vector.tensor_scalar(out=is0[:], in0=s_sb[:], scalar1=0.0, scalar2=TINY, op0=ALU.is_equal, op1=ALU.mult)
-            nc.vector.tensor_tensor(out=s_sb[:], in0=s_sb[:], in1=is0[:], op=ALU.add)
-            nc.vector.tensor_scalar(out=neg[:], in0=s_sb[:], scalar1=-1.0, scalar2=None, op0=ALU.mult)
-            nc.vector.reciprocal(out=rho[:], in_=s_sb[:])
-            nc.vector.tensor_tensor(out=hi[:], in0=s_sb[:], in1=neg[:], op=ALU.max)
-            nc.vector.tensor_tensor(out=rho[:], in0=rho[:], in1=c_sb[:], op=ALU.mult)
-            nc.vector.tensor_tensor(out=lo[:], in0=s_sb[:], in1=neg[:], op=ALU.min)
-
-        def tanh(k, ts):
-            if ("ph", k) not in pt:
-                pt["ph", k] = work.tile([128, 4, 512], F32, name=f"ph{k}", tag="ph", bufs=2)
-            nc.scalar.activation(out=pt["ph", k][:, ts, :], in_=ph_bank[k, ts][:], func=ACT.Tanh)
-
-        def scale(k, key, src, ts=None):
-            tg, h = chunks[k]
-            if ts is None:
-                for t4 in range(4):
-                    scale(k, key, src, t4)
-                return
-            if (key, k) not in pt:
-                pt[key, k] = work.tile([128, 4, 512], F32, name=f"{key}{k}", tag=key, bufs=1)
-            v = s_sb if key == src else rho
-            nc.scalar.activation(
-                out=pt[key, k][:, ts, :],
-                in_=pt[src, k][:, ts, :],
-                func=ACT.Copy,
-                scale=v[:, tg * 4 + ts : tg * 4 + ts + 1],
-            )
-
-        def r_view(o):
-            return o.rearrange("p (b m) t -> p m t b", b=4)
-
-        def r_src(i):
-            return i.rearrange("p t (m b) -> p m t b", b=4)
-
-        def r_join(k):
-            t = work.tile([128, 512, 4], BF16, name=f"r{k}", tag="r", bufs=1, align_bytes=64)
-            pt["r", k] = t
+        def join_l(k):
+            tiles["l", k] = work.tile([P, HALF, SLOTS], BF16, name=f"l{k}", tag="l", bufs=1, align_bytes=64)
             nc.vector.tensor_tensor(
-                out=r_view(t[:]), in0=r_src(pt["cp", k][:]), in1=r_src(pt["cph", k][:]), op=ALU.add
-            )
-
-        def e_sum(k):
-            e = work.tile([128, 512, 4], F32, name=f"e{k}", tag="e", bufs=1)
-            pt["e", k] = e
-            nc.vector.tensor_tensor(
-                out=e[:].rearrange("p (b m) t -> p m t b", b=4),
-                in0=pt["p", k][:].rearrange("p t (m b) -> p m t b", b=4),
-                in1=pt["ph", k][:].rearrange("p t (m b) -> p m t b", b=4),
-                op=ALU.add,
-            )
-
-        def r_mul(k):
-            tg, h = chunks[k]
-            t = work.tile([128, 512, 4], BF16, name=f"r{k}", tag="r", bufs=1, align_bytes=64)
-            pt["r", k] = t
-            nc.vector.tensor_tensor(
-                out=t[:],
-                in0=pt["e", k][:],
-                in1=rho[:, tg * 4 : tg * 4 + 4].unsqueeze(1).to_broadcast([128, 512, 4]),
-                op=ALU.mult,
-            )
-
-        def l_diff(k, lo=0, hi=512):
-            if ("l", k) not in pt:
-                pt["l", k] = work.tile([128, 512, 4], BF16, name=f"l{k}", tag="l", bufs=1, align_bytes=64)
-            t = pt["l", k]
-            nc.vector.tensor_tensor(
-                out=t[:, lo:hi].rearrange("p (c i) t -> p c t i", i=4),
-                in0=pt["p", k][:, :, lo:hi].rearrange("p t (c i) -> p c t i", i=4),
-                in1=pt["ph", k][:, :, lo:hi].rearrange("p t (c i) -> p c t i", i=4),
+                out=tiles["l", k][:].rearrange("p (c i) t -> p c t i", i=4),
+                in0=tiles["sp", k][:].rearrange("p t (c i) -> p c t i", i=4),
+                in1=tiles["sph", k][:].rearrange("p t (c i) -> p c t i", i=4),
                 op=ALU.subtract,
             )
 
-        def lr_quant(k, which, lo=0, hi=512):
-            tg, h = chunks[k]
-            codes, scales = (l_codes, l_scales) if which == "l" else (r_codes, r_scales)
+        def join_sum(k, a, b, out):
+            nc.vector.tensor_tensor(
+                out=out[:].rearrange("p (b m) t -> p m t b", b=4),
+                in0=tiles[a, k][:].rearrange("p t (m b) -> p m t b", b=4),
+                in1=tiles[b, k][:].rearrange("p t (m b) -> p m t b", b=4),
+                op=ALU.add,
+            )
+
+        def r_tile(k):
+            tiles["r", k] = work.tile([P, HALF, SLOTS], BF16, name=f"r{k}", tag="r", bufs=1, align_bytes=64)
+            return tiles["r", k]
+
+        def join_r(k):
+            join_sum(k, "c_from_sp", "c_from_sph", r_tile(k))
+
+        def sum_for_r(k):
+            tiles["sum", k] = work.tile([P, HALF, SLOTS], F32, name=f"sum{k}", tag="sum", bufs=1)
+            join_sum(k, "sp", "sph", tiles["sum", k])
+
+        def scale_r(k):
+            col = CHUNKS[k][0] * SLOTS
+            nc.vector.tensor_tensor(
+                out=r_tile(k)[:],
+                in0=tiles["sum", k][:],
+                in1=factors["ratio"][:, col : col + SLOTS].unsqueeze(1).to_broadcast([P, HALF, SLOTS]),
+                op=ALU.mult,
+            )
+
+        def quantise_lr(which, k):
+            blk, h = CHUNKS[k]
+            codes, scales = lr_mx[which]
+            cols = slice(h * HALF, (h + 1) * HALF)
             nc.vector.quantize_mx(
-                out=codes[:, tg, h * 512 + lo : h * 512 + hi].bitcast(FP8),
-                scales=scales[:, tg, h * 512 + lo : h * 512 + hi],
-                in_=pt[which, k][:, lo:hi].rearrange("p n t -> p (n t)"),
+                out=codes[:, blk, cols].bitcast(FP8),
+                scales=scales[:, blk, cols],
+                in_=tiles[which, k][:].rearrange("p n t -> p (n t)"),
             )
 
-        L = (l_codes, l_scales)
-        R = (r_codes, r_scales)
+        rows_bank = {}
+        rows_sb = {}
 
-        def mx(out, stat, scol, mov, mcol, width, tgs):
-            for tg in tgs:
-                nc.tensor.matmul_mx(
-                    out=out,
-                    lhsT=stat[0][:, tg, scol : scol + 128].bitcast(FP8),
-                    lhsT_scale=stat[1][:, tg, scol : scol + 128],
-                    rhs=mov[0][:, tg, mcol : mcol + width].bitcast(FP8),
-                    rhs_scale=mov[1][:, tg, mcol : mcol + width],
-                    start=(tg == 0),
-                    stop=(tg == 1),
-                )
-
-        def copy_scaled(o, i, eng):
-            if eng == V:
-                nc.vector.tensor_scalar(out=o, in0=i, scalar1=HEBB, scalar2=None, op0=ALU.mult)
-            else:
-                nc.scalar.activation(out=o, in_=i, func=ACT.Copy, scale=HEBB)
-
-        ob = {}
-        o_sb = {}
-
-        def out_first(i, h, tag):
-            ob[i, h] = bank(tag)
-            mx(ob[i, h][:], L, i * 128, R, h * 512, 512, (0,))
-
-        def out_second(i, h):
-            mx(ob[i, h][:], L, i * 128, R, h * 512, 512, (1,))
-
-        def out_mm(i, h, tag):
-            out_first(i, h, tag)
-            out_second(i, h)
-
-        def out_copy(i, h, eng):
-            o = work.tile([128, 512], F32, name=f"o{i}{h}", tag="o", bufs=9)
-            o_sb[i, h] = o
-            copy_scaled(
-                o[:].rearrange("p (m b) -> p m b", b=4), ob[i, h][:].rearrange("p (b m) -> p m b", b=4), eng
-            )
-            nc.sync.dma_start(out=out_0[i * 128 : (i + 1) * 128, h * 512 : (h + 1) * 512], in_=o[:])
-
-        planes = {}
-
-        def plane_tile(gb, ah):
-            if (gb, ah) not in planes:
-                planes[gb, ah] = work.tile([128, 512, 4], BF16, name=f"pb{gb}{ah}", tag="pb", bufs=2, align_bytes=64)
-            return planes[gb, ah]
-
-        def outT_mm(gb, j, tag):
-            b = bank(tag)
-            ob["T", gb, j] = b
-            for tb in range(4):
-                mx(b[:, tb * 128 : (tb + 1) * 128], R, gb * 512 + tb * 128, L, j * 128, 128, (0, 1))
-
-        def outT_copy(gb, j, eng):
-            copy_scaled(
-                plane_tile(gb, j // 4)[:, (j % 4) * 128 : (j % 4 + 1) * 128, :],
-                ob["T", gb, j][:].rearrange("p (b a) -> p a b", b=4),
-                eng,
+        def rows_pass(i, h, B, tag=None):
+            if tag is not None:
+                rows_bank[i, h] = bank(tag)
+            l_codes, l_scales = lr_mx["l"]
+            r_codes, r_scales = lr_mx["r"]
+            rows = slice(i * P, (i + 1) * P)
+            cols = slice(h * HALF, (h + 1) * HALF)
+            mx_pass(
+                rows_bank[i, h][:], l_codes[:, B, rows], l_scales[:, B, rows], r_codes[:, B, cols], r_scales[:, B, cols], B
             )
 
-        o16 = {}
+        def rows_product(i, h, tag):
+            rows_pass(i, h, 0, tag)
+            rows_pass(i, h, 1)
 
-        def conv(i, h, eng):
-            t = work.tile([128, 512], BF16, name=f"o16_{i}{h}", tag="o16", bufs=4)
-            o16[i, h] = t
-            if eng == G:
-                nc.gpsimd.tensor_scalar(out=t[:], in0=o_sb[i, h][:], scalar1=1.0, scalar2=0.0, op0=ALU.mult, op1=ALU.add)
-            elif eng == V:
-                nc.vector.tensor_copy(out=t[:], in_=o_sb[i, h][:])
-            else:
-                nc.scalar.copy(out=t[:], in_=o_sb[i, h][:])
-
-        def plane_turn(gb, pair, tag):
-            b = bank(tag)
-            ob["P", gb, pair] = b
-            for ii in range(2):
-                words = o16[2 * pair + ii, gb][:].bitcast(F32)
-                for u in range(2):
-                    kk = 2 * ii + u
-                    nc.tensor.transpose(b[:, kk * 128 : (kk + 1) * 128], words[:, u:256:2], ident[:])
-
-        def plane_copy(gb, pair, eng):
-            ah = pair // 2
-            t = plane_tile(gb, ah)[:].rearrange("p a t -> p (a t)").bitcast(F32)
-            o = t[:, (pair % 2) * 512 : (pair % 2 + 1) * 512].rearrange("p (i a u) -> p i a u", i=2, u=2)
-            i = ob["P", gb, pair][:].rearrange("p (i u a) -> p i a u", i=2, u=2)
-            if eng == V:
-                nc.vector.tensor_copy(out=o, in_=i)
-            else:
-                nc.scalar.copy(out=o, in_=i)
-
-        pl_scales = [keep.tile([128, N], U8, name=f"pl_scales{gb}", align_bytes=64) for gb in range(2)]
-
-        def plane_quant(gb, ah):
-            w = work.tile([128, 512], U32, name=f"pw{gb}{ah}", tag=f"pw{gb}{ah}", bufs=1, align_bytes=64)
-            nc.vector.quantize_mx(
-                out=w[:].bitcast(FP8),
-                scales=pl_scales[gb][:, ah * 512 : (ah + 1) * 512],
-                in_=planes[gb, ah][:].rearrange("p a t -> p (a t)"),
+        def rows_out(i, h, engine):
+            rows_sb[i, h] = work.tile([P, HALF], F32, name=f"rows{i}{h}", tag="rows", bufs=9)
+            copy_times_hebb(
+                engine,
+                out=rows_sb[i, h][:].rearrange("p (m b) -> p m b", b=4),
+                in_=rows_bank[i, h][:].rearrange("p (b m) -> p m b", b=4),
             )
             nc.sync.dma_start(
-                out=out_1[gb].rearrange("p a t -> p (a t)")[:, ah * 2048 : (ah + 1) * 2048].bitcast(I32),
-                in_=w[:].bitcast(I32),
+                out=out_0[i * P : (i + 1) * P, h * HALF : (h + 1) * HALF], in_=rows_sb[i, h][:]
+            )
+
+        plane_in = {}
+        plane_bank = {}
+
+        def plane_tile(G, e):
+            if (G, e) not in plane_in:
+                plane_in[G, e] = work.tile(
+                    [P, HALF, SLOTS], BF16, name=f"plane{G}{e}", tag="plane", bufs=2, align_bytes=64
+                )
+            return plane_in[G, e]
+
+        def plane_product(G, i, tag):
+            plane_bank[G, i] = bank(tag)
+            l_codes, l_scales = lr_mx["l"]
+            r_codes, r_scales = lr_mx["r"]
+            cols = slice(i * P, (i + 1) * P)
+            for t in range(SLOTS):
+                rows = slice(G * HALF + t * P, G * HALF + (t + 1) * P)
+                for B in range(2):
+                    mx_pass(
+                        plane_bank[G, i][:, t * P : (t + 1) * P],
+                        r_codes[:, B, rows],
+                        r_scales[:, B, rows],
+                        l_codes[:, B, cols],
+                        l_scales[:, B, cols],
+                        B,
+                    )
+
+        def plane_copy(G, i, engine):
+            at = (i % 4) * P
+            copy_times_hebb(
+                engine,
+                out=plane_tile(G, i // 4)[:, at : at + P, :],
+                in_=plane_bank[G, i][:].rearrange("p (t a) -> p a t", t=SLOTS),
+            )
+
+        rounded = {}
+
+        def round_rows(i, h, engine):
+            rounded[i, h] = work.tile([P, HALF], BF16, name=f"rounded{i}{h}", tag="rounded", bufs=4)
+            copy(engine, out=rounded[i, h][:], in_=rows_sb[i, h][:])
+
+        def transpose_out(G, pair, tag):
+            plane_bank["pair", G, pair] = bank(tag)
+            for a in range(2):
+                words = rounded[2 * pair + a, G][:].bitcast(F32)
+                for u in range(2):
+                    at = (2 * a + u) * P
+                    nc.tensor.transpose(plane_bank["pair", G, pair][:, at : at + P], words[:, u:256:2], ident[:])
+
+        def plane_from_rows(G, pair, engine):
+            words = plane_tile(G, pair // 2)[:].rearrange("p a t -> p (a t)").bitcast(F32)
+            at = (pair % 2) * HALF
+            copy(
+                engine,
+                out=words[:, at : at + HALF].rearrange("p (i a u) -> p i a u", i=2, u=2),
+                in_=plane_bank["pair", G, pair][:].rearrange("p (i u a) -> p i a u", i=2, u=2),
+            )
+
+        def planes_out(G, e):
+            cols = slice(e * HALF, (e + 1) * HALF)
+            words = work.tile([P, HALF], U32, name=f"words{G}{e}", tag="words", bufs=4, align_bytes=64)
+            nc.vector.quantize_mx(
+                out=words[:].bitcast(FP8),
+                scales=plane_scales[G][:, cols],
+                in_=plane_in[G, e][:].rearrange("p a t -> p (a t)"),
+            )
+            nc.sync.dma_start(
+                out=out_1[G].rearrange("p a t -> p (a t)")[:, e * 4 * HALF : (e + 1) * 4 * HALF].bitcast(I32),
+                in_=words[:].bitcast(I32),
             )
             for Q in range(4):
                 nc.sync.dma_start(
-                    out=out_2[gb, 4 * Q : 4 * Q + 4, ah * 512 : (ah + 1) * 512].bitcast(I32),
-                    in_=pl_scales[gb][32 * Q : 32 * Q + 4, ah * 512 : (ah + 1) * 512].bitcast(I32),
+                    out=out_2[G, 4 * Q : 4 * Q + 4, cols].bitcast(I32),
+                    in_=plane_scales[G][32 * Q : 32 * Q + 4, cols].bitcast(I32),
                 )
 
-        def turn_mms(mat, tg, a, b):
-            for ts in range(a, b):
-                turn_mm(mat, tg, ts)
-
-        def turn_copies(mat, tg, a, b, eng):
-            for ts in range(a, b):
-                turn_copy(mat, tg, ts, eng)
-
-        def gts(k, a, b):
-            for ts in range(a, b):
-                mm_gt(k, ts)
-
-        def phs(k, a, b):
-            for ts in range(a, b):
-                mm_ph(k, ts)
-
-        def gate(k, a, b, eng):
-            for ts in range(a, b):
-                y(k, ts)
-                if eng == G:
-                    clamp(k, ts, G)
-            if eng != G:
-                for ts in range(a, b):
-                    clamp(k, ts, eng)
-
-        def tanhs(k, a, b):
-            for ts in range(a, b):
-                tanh(k, ts)
-
-        def scales(k, key, src, a, b):
-            for ts in range(a, b):
-                scale(k, key, src, ts)
-
-        turn_mms("q", 0, 0, 2)
-        prep()
-        turn_copies("q", 0, 1, 2, V)
-        turn_mms("q", 0, 2, 4)
-        turn_copies("q", 0, 2, 3, V)
-        turn_copies("q", 0, 0, 1, S)
-        turn_mms("g", 0, 0, 2)
-        turn_copies("q", 0, 3, 4, V)
-        act_quant("q", 0, 1)
-        turn_copies("g", 0, 0, 1, S)
-        m0_il(0, 0, S)
-        act_quant("q", 0, 0)
-        turn_copies("g", 0, 1, 2, V)
-        act_quant("g", 0, 0)
-        m0_il(0, 1, V)
-        turn_mms("g", 0, 2, 4)
-        m0_quant(0, 0)
-        m0_quant(0, 1)
-        gts(0, 0, 2)
-        turn_copies("g", 0, 3, 4, S)
-        turn_copies("g", 0, 2, 3, S)
-        act_quant("g", 0, 1)
-        phs(0, 0, 2)
+        factors_ready()
+        transpose_rows("q", 0, 0, 2)
+        group_rows("q", 0, 0, 2, SCALAR)
+        transpose_rows("q", 0, 2, 4)
+        group_rows("q", 0, 3, 4, VECTOR)
+        quantise_rows("q", 0, 0)
+        group_rows("q", 0, 2, 3, SCALAR)
+        quantise_rows("q", 0, 1)
+        transpose_rows("g", 0, 0, 2)
+        group_rows("g", 0, 0, 1, SCALAR)
+        group_rows("g", 0, 1, 2, VECTOR)
+        group_m0(0, 0, SCALAR)
+        transpose_rows("g", 0, 2, 4)
+        group_rows("g", 0, 3, 4, SCALAR)
+        quantise_rows("g", 0, 0)
+        products_gate(0, 0, 2)
+        group_m0(0, 1, VECTOR)
+        quantise_m0(0, 0)
+        quantise_m0(0, 1)
+        products_tanh(0, 0, 2)
+        group_rows("g", 0, 2, 3, SCALAR)
         tanhs(0, 0, 2)
-        phs(0, 2, 4)
+        times_s(0, 0, 2)
+        quantise_rows("g", 0, 1)
+        products_gate(0, 2, 4)
+        gate(0, 0, 2)
+        gate(0, 2, 4)
+        products_tanh(0, 2, 4)
+        transpose_rows("g", 1, 0, 2)
+        group_rows("g", 1, 1, 2, VECTOR)
         tanhs(0, 2, 4)
-        gate(0, 0, 2, G)
-        scales(0, "ph", "ph", 2, 4)
-        scales(0, "ph", "ph", 0, 2)
-        gts(0, 2, 4)
-        gate(0, 2, 4, G)
-        turn_mms("g", 1, 0, 2)
-        turn_copies("g", 1, 0, 1, V)
-        turn_copies("g", 1, 1, 2, V)
-        act_quant("g", 1, 0)
-        e_sum(0)
-        turn_mms("g", 1, 2, 4)
-        turn_copies("g", 1, 2, 3, S)
-        turn_copies("g", 1, 3, 4, S)
-        act_quant("g", 1, 1)
-        turn_mms("q", 1, 0, 2)
-        r_mul(0)
-        gts(1, 0, 2)
-        turn_copies("q", 1, 1, 2, S)
-        turn_copies("q", 1, 0, 1, S)
-        act_quant("q", 1, 0)
-        turn_mms("q", 1, 2, 4)
-        turn_copies("q", 1, 3, 4, S)
-        l_diff(0)
-        phs(1, 0, 2)
-        gate(1, 0, 2, G)
-        gts(1, 2, 4)
-        gate(1, 2, 4, G)
-        gts(2, 0, 2)
-        turn_copies("q", 1, 2, 3, S)
-        gate(2, 0, 2, G)
-        act_quant("q", 1, 1)
-        gts(2, 2, 4)
-        phs(1, 2, 4)
+        times_s(0, 2, 4)
+        join_l(0)
+        sum_for_r(0)
+        group_rows("g", 1, 0, 1, SCALAR)
+        quantise_rows("g", 1, 0)
+        transpose_rows("g", 1, 2, 4)
+        group_rows("g", 1, 2, 4, SCALAR)
+        quantise_rows("g", 1, 1)
+        scale_r(0)
+        transpose_rows("q", 1, 0, 2)
+        group_rows("q", 1, 1, 2, SCALAR)
+        group_rows("q", 1, 0, 1, SCALAR)
+        products_gate(1, 0, 2)
+        quantise_rows("q", 1, 0)
+        gate(1, 0, 2)
+        group_m0(1, 0, SCALAR)
+        transpose_rows("q", 1, 2, 4)
+        products_gate(1, 2, 4)
+        products_tanh(1, 0, 2)
+        group_rows("q", 1, 3, 4, SCALAR)
+        gate(1, 2, 4)
+        group_rows("q", 1, 2, 3, SCALAR)
         tanhs(1, 0, 2)
-        m0_il(1, 1, V)
-        m0_il(1, 0, S)
-        scales(1, "ph", "ph", 0, 2)
-        scales(1, "cph", "ph", 0, 2)
-        scales(1, "cp", "p", 2, 4)
-        gate(2, 2, 4, G)
-        m0_quant(1, 0)
+        times_s(1, 0, 2)
+        quantise_rows("q", 1, 1)
+        products_gate(2, 0, 2)
+        gate(2, 0, 2)
+        quantise_lr("r", 0)
+        products_tanh(1, 2, 4)
         tanhs(1, 2, 4)
-        m0_quant(1, 1)
-        scales(1, "ph", "ph", 2, 4)
-        lr_quant(0, "l")
-        gts(3, 0, 2)
-        scales(1, "cph", "ph", 2, 4)
-        scales(1, "cp", "p", 0, 2)
-        phs(2, 0, 2)
-        lr_quant(0, "r")
-        l_diff(1)
+        times_s(1, 2, 4)
+        times_ratio(1, "sp", 2, 4)
+        quantise_lr("l", 0)
+        group_m0(1, 1, VECTOR)
+        quantise_m0(1, 0)
+        products_gate(2, 2, 4)
+        quantise_m0(1, 1)
+        gate(2, 2, 4)
+        times_ratio(1, "sph", 2, 4)
+        products_gate(3, 0, 2)
+        products_tanh(2, 0, 2)
+        times_ratio(1, "sph", 0, 2)
+        join_l(1)
+        times_ratio(1, "sp", 0, 2)
+        products_tanh(2, 2, 4)
         tanhs(2, 0, 2)
-        scales(2, "ph", "ph", 0, 2)
-        r_join(1)
-        lr_quant(1, "l")
-        phs(2, 2, 4)
+        join_r(1)
+        products_tanh(3, 0, 2)
+        products_gate(3, 2, 4)
+        gate(3, 0, 2)
         tanhs(2, 2, 4)
-        scales(2, "ph", "ph", 2, 4)
-        gate(3, 0, 2, G)
-        lr_quant(1, "r")
-        phs(3, 0, 2)
+        times_s(2, 2, 4)
+        quantise_lr("r", 1)
+        times_s(2, 0, 2)
         tanhs(3, 0, 2)
-        gts(3, 2, 4)
-        gate(3, 2, 4, G)
-        out_mm(1, 0, "t")
-        out_mm(2, 0, "t")
-        phs(3, 2, 4)
-        l_diff(2)
-        e_sum(2)
-        scales(3, "ph", "ph", 0, 2)
-        scales(3, "cp", "p", 0, 2)
+        times_s(3, 0, 2)
+        products_tanh(3, 2, 4)
         tanhs(3, 2, 4)
-        scales(3, "ph", "ph", 2, 4)
-        out_copy(2, 0, S)
-        scales(3, "cph", "ph", 0, 2)
-        out_copy(1, 0, V)
-        outT_mm(0, 2, "s")
-        outT_copy(0, 2, S)
-        r_mul(2)
-        lr_quant(2, "r")
-        out_mm(0, 0, "t")
-        scales(3, "cph", "ph", 2, 4)
-        out_copy(0, 0, S)
-        scales(3, "cp", "p", 2, 4)
-        outT_mm(0, 3, "s")
-        outT_copy(0, 3, S)
-        lr_quant(2, "l")
-        outT_mm(0, 1, "t")
-        outT_mm(0, 0, "t")
-        outT_copy(0, 0, S)
-        outT_copy(0, 1, S)
-        r_join(3)
-        out_first(6, 0, "v")
-        out_first(5, 0, "v")
-        lr_quant(3, "r")
-        out_mm(3, 0, "t")
-        out_copy(3, 0, S)
-        out_mm(0, 1, "t")
-        out_copy(0, 1, S)
-        out_mm(1, 1, "s")
-        out_first(4, 0, "v")
-        l_diff(3)
-        out_mm(2, 1, "t")
-        out_copy(1, 1, S)
-        lr_quant(3, "l")
-        out_copy(2, 1, S)
-        plane_quant(0, 0)
-        outT_mm(1, 2, "s")
-        outT_copy(1, 2, V)
-        outT_mm(1, 1, "t")
-        out_second(6, 0)
-        out_second(5, 0)
-        out_second(4, 0)
-        out_copy(5, 0, V)
-        out_copy(6, 0, S)
-        outT_copy(1, 1, S)
-        outT_mm(1, 3, "t")
-        out_mm(7, 0, "v")
-        conv(5, 0, V)
-        out_copy(7, 0, S)
-        out_mm(5, 1, "v")
-        out_copy(4, 0, V)
-        out_copy(5, 1, S)
-        outT_copy(1, 3, V)
-        outT_mm(1, 0, "t")
-        outT_copy(1, 0, S)
-        conv(4, 0, V)
-        conv(7, 0, S)
-        conv(6, 0, V)
-        plane_quant(1, 0)
-        out_mm(7, 1, "s")
-        out_copy(7, 1, S)
-        out_mm(4, 1, "v")
-        out_copy(4, 1, V)
-        out_mm(6, 1, "t")
-        out_copy(6, 1, V)
-        plane_turn(0, 2, "t")
-        plane_turn(0, 3, "s")
-        plane_copy(0, 3, S)
-        plane_copy(0, 2, V)
-        outT_mm(1, 5, "v")
-        plane_quant(0, 1)
-        outT_mm(1, 4, "t")
-        outT_copy(1, 4, V)
-        out_mm(3, 1, "s")
-        out_copy(3, 1, S)
-        outT_mm(1, 7, "v")
-        outT_copy(1, 7, S)
-        outT_mm(1, 6, "v")
-        outT_copy(1, 6, S)
-        outT_copy(1, 5, V)
-        plane_quant(1, 1)
+        times_s(3, 2, 4)
+        times_ratio(3, "sph", 2, 4)
+        quantise_lr("l", 1)
+        rows_product(1, 0, "turn")
+        plane_product(0, 3, "gate")
+        times_ratio(3, "sp", 0, 2)
+        gate(3, 2, 4)
+        rows_product(2, 0, "turn")
+        plane_product(0, 0, "gate")
+        rows_product(0, 0, "tanh")
+        join_l(2)
+        plane_product(0, 2, "tanh")
+        times_ratio(3, "sph", 0, 2)
+        plane_product(0, 1, "turn")
+        rows_out(1, 0, SCALAR)
+        sum_for_r(2)
+        plane_copy(0, 2, SCALAR)
+        times_ratio(3, "sp", 2, 4)
+        scale_r(2)
+        quantise_lr("r", 2)
+        rows_out(2, 0, SCALAR)
+        plane_copy(0, 3, SCALAR)
+        rows_product(3, 0, "turn")
+        plane_copy(0, 1, SCALAR)
+        quantise_lr("l", 2)
+        rows_pass(5, 0, 0, "turn")
+        rows_out(0, 0, SCALAR)
+        plane_copy(0, 0, SCALAR)
+        rows_pass(4, 0, 0, "gate")
+        join_r(3)
+        rows_pass(6, 0, 0, "gate")
+        quantise_lr("r", 3)
+        rows_product(2, 1, "tanh")
+        rows_out(3, 0, SCALAR)
+        rows_out(2, 1, SCALAR)
+        rows_product(1, 1, "gate")
+        rows_product(0, 1, "tanh")
+        rows_out(0, 1, SCALAR)
+        rows_out(1, 1, SCALAR)
+        plane_product(1, 1, "tanh")
+        join_l(3)
+        plane_product(1, 2, "tanh")
+        quantise_lr("l", 3)
+        rows_product(7, 0, "turn")
+        planes_out(0, 0)
+        rows_pass(5, 0, 1)
+        rows_out(5, 0, VECTOR)
+        rows_pass(6, 0, 1)
+        rows_out(7, 0, SCALAR)
+        round_rows(7, 0, VECTOR)
+        rows_pass(4, 0, 1)
+        plane_copy(1, 2, VECTOR)
+        plane_product(1, 3, "tanh")
+        plane_product(1, 0, "turn")
+        rows_product(7, 1, "tanh")
+        plane_copy(1, 1, SCALAR)
+        rows_out(6, 0, SCALAR)
+        round_rows(6, 0, VECTOR)
+        rows_product(6, 1, "tanh")
+        plane_copy(1, 3, SCALAR)
+        rows_product(4, 1, "turn")
+        plane_copy(1, 0, VECTOR)
+        round_rows(5, 0, VECTOR)
+        rows_out(4, 0, SCALAR)
+        planes_out(1, 0)
+        round_rows(4, 0, SCALAR)
+        rows_product(5, 1, "gate")
+        rows_out(5, 1, VECTOR)
+        transpose_out(0, 3, "turn")
+        plane_from_rows(0, 3, VECTOR)
+        rows_out(7, 1, SCALAR)
+        transpose_out(0, 2, "gate")
+        rows_out(6, 1, VECTOR)
+        plane_from_rows(0, 2, SCALAR)
+        planes_out(0, 1)
+        plane_product(1, 6, "tanh")
+        plane_product(1, 7, "tanh")
+        plane_copy(1, 7, VECTOR)
+        plane_copy(1, 6, SCALAR)
+        rows_out(4, 1, SCALAR)
+        plane_product(1, 5, "gate")
+        plane_product(1, 4, "gate")
+        plane_copy(1, 5, VECTOR)
+        plane_copy(1, 4, VECTOR)
+        rows_product(3, 1, "gate")
+        rows_out(3, 1, SCALAR)
+        planes_out(1, 1)

from contextlib import ExitStack

import concourse.mybir as mybir
from concourse.masks import make_identity

N = 1024
HALF = 512
P = 128
SLOTS = 4
HEBB = 0.03125
TINY = 2.0**-100
FLOPS = 3 * 2 * N * N * N

F32 = mybir.dt.float32
BF16 = mybir.dt.bfloat16
U32 = mybir.dt.uint32
I32 = mybir.dt.int32
U8 = mybir.dt.uint8
FP8 = mybir.dt.float8_e4m3fn_x4
FP4 = mybir.dt.float4_e2m1fn_x4
ALU = mybir.AluOpType
ACT = mybir.ActivationFunctionType

VECTOR, SCALAR = "vector", "scalar"

BANKS = {"turn": 2, "tanh": 3, "gate": 3}
CHUNKS = ((0, 0), (1, 0), (0, 1), (1, 1))


def tile_differencesumouterproduct_kernel(tc, g, wg_words, wg_scales, x, q, m0, s, c, out_0, out_1, out_2):
    nc = tc.nc
    with ExitStack() as ctx:
        keep = ctx.enter_context(tc.tile_pool(name="keep", bufs=1))
        work = ctx.enter_context(tc.tile_pool(name="work", bufs=1))
        psum = ctx.enter_context(tc.psum_pool(name="psum", bufs=1))
        ctx.enter_context(tc.manual_schedule())

        def codes_and_scales(shape, name):
            codes = keep.tile([P] + shape, U32, name=name + "_codes", align_bytes=64)
            scales = keep.tile([P] + shape, U8, name=name + "_scales", align_bytes=64)
            return codes, scales

        ident = keep.tile([P, P], F32, name="ident")
        wg_sb = [keep.tile([P, 2, 2 * HALF], U8, name=f"wg{h}", align_bytes=64) for h in range(2)]
        wg_sc = keep.tile([P, 2, N], U8, name="wg_sc", align_bytes=64)
        acts = {(mat, blk): codes_and_scales([SLOTS, 2, P], f"{mat}{blk}") for mat in ("g", "q") for blk in range(2)}
        m0_mx = codes_and_scales([2, N], "m0")
        lr_mx = {which: codes_and_scales([2, N], which) for which in ("l", "r")}
        plane_scales = [keep.tile([P, N], U8, name=f"plane_scales{G}", align_bytes=64) for G in range(2)]

        factors = {}
        for name, vec in (("s", s), ("c", c)):
            factors[name] = keep.tile([P, 2 * SLOTS], BF16, name=name + "_raw")
            nc.scalar.dma_start(
                out=factors[name][:].rearrange("p (b t) -> p b t", b=2),
                in_=vec.rearrange("(b p t) -> p b t", b=2, t=SLOTS),
            )
        zero = keep.tile([P, 1], F32, name="zero")
        nc.vector.memset(zero[:], 0.0)
        nc.scalar.activation(out=zero[:], in_=zero[:], func=ACT.Tanh)
        nc.gpsimd.memset(wg_sc[:].rearrange("p g n -> p (g n)").bitcast(I32), 0)
        make_identity(nc, ident[:])

        raw = {}

        def load_rows(mat, src, blk, pieces):
            raw[mat, blk] = work.tile([P, SLOTS, N], BF16, name=f"{mat}_raw{blk}", tag="raw", bufs=4)
            rows = src.rearrange("(b m t) k -> b m t k", b=2, t=SLOTS)[blk]
            step = SLOTS // pieces
            for t in range(0, SLOTS, step):
                nc.sync.dma_start(out=raw[mat, blk][:, t : t + step], in_=rows[:, t : t + step])

        def load_m0(h):
            raw["m0", h] = work.tile([P, 2, SLOTS, HALF], BF16, name=f"m0_raw{h}", tag="raw", bufs=4)
            rows = m0.rearrange("(g p t) n -> g p t n", g=2, t=SLOTS)
            for G in range(2):
                nc.sync.dma_start(out=raw["m0", h][:, G], in_=rows[G, :, :, h * HALF : (h + 1) * HALF])

        def load_x(blk, h):
            raw["x", blk, h] = work.tile([P, SLOTS, HALF], BF16, name=f"x_raw{blk}{h}", tag="x", bufs=3)
            rows = x.rearrange("(b m t) n -> b m t n", b=2, t=SLOTS)[blk]
            nc.sync.dma_start(out=raw["x", blk, h][:], in_=rows[:, :, h * HALF : (h + 1) * HALF])

        def load_wg(h):
            nc.sync.dma_start(
                out=wg_sb[h][:].bitcast(I32),
                in_=wg_words[:, :, 2 * h * HALF : 2 * (h + 1) * HALF].rearrange("g p b -> p g b").bitcast(I32),
            )

        load_rows("q", q, 0, pieces=4)
        load_rows("g", g, 0, pieces=4)
        for Q in range(4):
            nc.sync.dma_start(
                out=wg_sc[32 * Q : 32 * Q + 4].bitcast(I32),
                in_=wg_scales[:, 4 * Q : 4 * Q + 4, :].rearrange("g r n -> r g n").bitcast(I32),
            )
        load_m0(0)
        load_wg(0)
        load_x(0, 0)
        load_rows("g", g, 1, pieces=2)
        load_rows("q", q, 1, pieces=2)
        load_x(1, 0)
        load_m0(1)
        load_wg(1)
        load_x(0, 1)
        load_x(1, 1)

        def bank(tag):
            return psum.tile([P, HALF], F32, name="bank_" + tag, tag=tag, bufs=BANKS[tag])

        def copy(engine, out, in_):
            if engine == VECTOR:
                nc.vector.tensor_copy(out=out, in_=in_)
            else:
                nc.scalar.copy(out=out, in_=in_)

        def copy_times_hebb(engine, out, in_):
            if engine == VECTOR:
                nc.vector.tensor_scalar(out=out, in0=in_, scalar1=HEBB, scalar2=None, op0=ALU.mult)
            else:
                nc.scalar.activation(out=out, in_=in_, func=ACT.Copy, scale=HEBB)

        def mx_pass(out, lhsT, lhsT_scale, rhs, rhs_scale, G, rhs_dtype=FP8):
            nc.tensor.matmul_mx(
                out=out,
                lhsT=lhsT.bitcast(FP8),
                lhsT_scale=lhsT_scale,
                rhs=rhs.bitcast(rhs_dtype),
                rhs_scale=rhs_scale,
                start=(G == 0),
                stop=(G == 1),
            )

        def factors_ready():
            def column_tile(name):
                factors[name] = keep.tile([P, 2 * SLOTS], F32, name=name)
                return factors[name][:]

            s32, c32, is_zero, minus = [column_tile(name) for name in ("s32", "c32", "is_zero", "minus")]
            ratio, high, low = [column_tile(name) for name in ("ratio", "high", "low")]
            nc.vector.tensor_copy(out=s32, in_=factors["s"][:])
            nc.vector.tensor_copy(out=c32, in_=factors["c"][:])
            nc.vector.tensor_scalar(out=is_zero, in0=s32, scalar1=0.0, scalar2=TINY, op0=ALU.is_equal, op1=ALU.mult)
            nc.vector.tensor_tensor(out=s32, in0=s32, in1=is_zero, op=ALU.add)
            nc.vector.tensor_scalar(out=minus, in0=s32, scalar1=-1.0, scalar2=None, op0=ALU.mult)
            nc.vector.reciprocal(out=ratio, in_=s32)
            nc.vector.tensor_tensor(out=high, in0=s32, in1=minus, op=ALU.max)
            nc.vector.tensor_tensor(out=ratio, in0=ratio, in1=c32, op=ALU.mult)
            nc.vector.tensor_tensor(out=low, in0=s32, in1=minus, op=ALU.min)

        def factor(name, k, t):
            column = CHUNKS[k][0] * SLOTS + t
            return factors[name][:, column : column + 1]

        grouped = {}
        turned = {}

        def grouped_tile(key, name):
            if key not in grouped:
                grouped[key] = work.tile([P, HALF * SLOTS], BF16, name=name, tag="grouped", bufs=5, align_bytes=64)
            return grouped[key]

        def transpose_rows(mat, blk, first, last):
            for t in range(first, last):
                turned[mat, blk, t] = bank("turn")
                words = raw[mat, blk][:, t, :].bitcast(F32)
                for G in range(2):
                    for u in range(2):
                        at = (2 * G + u) * P
                        nc.tensor.transpose(
                            turned[mat, blk, t][:, at : at + P], words[:, 256 * G + u : 256 * (G + 1) : 2], ident[:]
                        )

        def group_rows(mat, blk, first, last, engine):
            for t in range(first, last):
                tile = grouped_tile((mat, blk, t // 2), f"{mat}_grouped{blk}{t // 2}")
                words = tile[:].bitcast(F32)[:, (t % 2) * HALF : (t % 2 + 1) * HALF]
                copy(
                    engine,
                    out=words.rearrange("p (g m u) -> p g m u", g=2, u=2),
                    in_=turned[mat, blk, t][:].rearrange("p (g u m) -> p g m u", g=2, u=2),
                )

        def quantise_rows(mat, blk, pair):
            codes, scales = acts[mat, blk]
            both = slice(2 * pair, 2 * pair + 2)
            nc.vector.quantize_mx(
                out=codes[:, both].rearrange("p t g m -> p (t g m)").bitcast(FP8),
                scales=scales[:, both].rearrange("p t g m -> p (t g m)"),
                in_=grouped[mat, blk, pair][:],
            )

        def group_m0(h, G, engine):
            copy(
                engine,
                out=grouped_tile(("m0", h, G), f"m0_grouped{h}{G}")[:].rearrange("p (c i t) -> p c t i", i=4, t=SLOTS),
                in_=raw["m0", h][:, G].rearrange("p t (c i) -> p c t i", i=4),
            )

        def quantise_m0(h, G):
            codes, scales = m0_mx
            cols = slice(h * HALF, (h + 1) * HALF)
            nc.vector.quantize_mx(
                out=codes[:, G, cols].bitcast(FP8), scales=scales[:, G, cols], in_=grouped["m0", h, G][:]
            )

        product = {}
        tiles = {}

        def chunk_tile(key, k, bufs):
            if (key, k) not in tiles:
                tiles[key, k] = work.tile([P, SLOTS, HALF], F32, name=f"{key}{k}", tag=key, bufs=bufs)
            return tiles[key, k]

        def products_gate(k, first, last):
            blk, h = CHUNKS[k]
            codes, scales = acts["g", blk]
            for t in range(first, last):
                product["gate", k, t] = bank("gate")
                for G in range(2):
                    mx_pass(
                        product["gate", k, t][:],
                        codes[:, t, G, :],
                        scales[:, t, G, :],
                        wg_sb[h][:, G, :],
                        wg_sc[:, G, h * HALF : (h + 1) * HALF],
                        G,
                        rhs_dtype=FP4,
                    )

        def products_tanh(k, first, last):
            blk, h = CHUNKS[k]
            codes, scales = acts["q", blk]
            for t in range(first, last):
                product["tanh", k, t] = bank("tanh")
                for G in range(2):
                    mx_pass(
                        product["tanh", k, t][:],
                        codes[:, t, G, :],
                        scales[:, t, G, :],
                        m0_mx[0][:, G, h * HALF : (h + 1) * HALF],
                        m0_mx[1][:, G, h * HALF : (h + 1) * HALF],
                        G,
                    )

        def gate(k, first, last):
            blk, h = CHUNKS[k]
            sp = chunk_tile("sp", k, bufs=2)
            for t in range(first, last):
                nc.vector.scalar_tensor_tensor(
                    out=sp[:, t, :],
                    in0=product["gate", k, t][:],
                    scalar=factor("s32", k, t),
                    in1=raw["x", blk, h][:, t, :],
                    op0=ALU.mult,
                    op1=ALU.mult,
                )
                nc.gpsimd.tensor_scalar(
                    out=sp[:, t, :],
                    in0=sp[:, t, :],
                    scalar1=factor("high", k, t),
                    scalar2=factor("low", k, t),
                    op0=ALU.min,
                    op1=ALU.max,
                )

        def tanhs(k, first, last):
            sph = chunk_tile("sph", k, bufs=2)
            for t in range(first, last):
                nc.scalar.activation(out=sph[:, t, :], in_=product["tanh", k, t][:], func=ACT.Tanh, bias=zero[:])

        def times_s(k, first, last):
            sph = tiles["sph", k]
            for t in range(first, last):
                nc.scalar.activation(out=sph[:, t, :], in_=sph[:, t, :], func=ACT.Copy, scale=factor("s32", k, t))

        def times_ratio(k, src, first, last):
            out = chunk_tile("c_from_" + src, k, bufs=1)
            for t in range(first, last):
                nc.scalar.activation(
                    out=out[:, t, :], in_=tiles[src, k][:, t, :], func=ACT.Copy, scale=factor("ratio", k, t)
                )

        def join_l(k):
            tiles["l", k] = work.tile([P, HALF, SLOTS], BF16, name=f"l{k}", tag="l", bufs=1, align_bytes=64)
            nc.vector.tensor_tensor(
                out=tiles["l", k][:].rearrange("p (c i) t -> p c t i", i=4),
                in0=tiles["sp", k][:].rearrange("p t (c i) -> p c t i", i=4),
                in1=tiles["sph", k][:].rearrange("p t (c i) -> p c t i", i=4),
                op=ALU.subtract,
            )

        def join_sum(k, a, b, out):
            nc.vector.tensor_tensor(
                out=out[:].rearrange("p (b m) t -> p m t b", b=4),
                in0=tiles[a, k][:].rearrange("p t (m b) -> p m t b", b=4),
                in1=tiles[b, k][:].rearrange("p t (m b) -> p m t b", b=4),
                op=ALU.add,
            )

        def r_tile(k):
            tiles["r", k] = work.tile([P, HALF, SLOTS], BF16, name=f"r{k}", tag="r", bufs=1, align_bytes=64)
            return tiles["r", k]

        def join_r(k):
            join_sum(k, "c_from_sp", "c_from_sph", r_tile(k))

        def sum_for_r(k):
            tiles["sum", k] = work.tile([P, HALF, SLOTS], F32, name=f"sum{k}", tag="sum", bufs=1)
            join_sum(k, "sp", "sph", tiles["sum", k])

        def scale_r(k):
            col = CHUNKS[k][0] * SLOTS
            nc.vector.tensor_tensor(
                out=r_tile(k)[:],
                in0=tiles["sum", k][:],
                in1=factors["ratio"][:, col : col + SLOTS].unsqueeze(1).to_broadcast([P, HALF, SLOTS]),
                op=ALU.mult,
            )

        def quantise_lr(which, k):
            blk, h = CHUNKS[k]
            codes, scales = lr_mx[which]
            cols = slice(h * HALF, (h + 1) * HALF)
            nc.vector.quantize_mx(
                out=codes[:, blk, cols].bitcast(FP8),
                scales=scales[:, blk, cols],
                in_=tiles[which, k][:].rearrange("p n t -> p (n t)"),
            )

        rows_bank = {}
        rows_sb = {}

        def rows_pass(i, h, B, tag=None):
            if tag is not None:
                rows_bank[i, h] = bank(tag)
            l_codes, l_scales = lr_mx["l"]
            r_codes, r_scales = lr_mx["r"]
            rows = slice(i * P, (i + 1) * P)
            cols = slice(h * HALF, (h + 1) * HALF)
            mx_pass(
                rows_bank[i, h][:], l_codes[:, B, rows], l_scales[:, B, rows], r_codes[:, B, cols], r_scales[:, B, cols], B
            )

        def rows_product(i, h, tag):
            rows_pass(i, h, 0, tag)
            rows_pass(i, h, 1)

        def rows_out(i, h, engine):
            rows_sb[i, h] = work.tile([P, HALF], F32, name=f"rows{i}{h}", tag="rows", bufs=9)
            copy_times_hebb(
                engine,
                out=rows_sb[i, h][:].rearrange("p (m b) -> p m b", b=4),
                in_=rows_bank[i, h][:].rearrange("p (b m) -> p m b", b=4),
            )
            nc.sync.dma_start(
                out=out_0[i * P : (i + 1) * P, h * HALF : (h + 1) * HALF], in_=rows_sb[i, h][:]
            )

        plane_in = {}
        plane_bank = {}

        def plane_tile(G, e):
            if (G, e) not in plane_in:
                plane_in[G, e] = work.tile(
                    [P, HALF, SLOTS], BF16, name=f"plane{G}{e}", tag="plane", bufs=2, align_bytes=64
                )
            return plane_in[G, e]

        def plane_product(G, i, tag):
            plane_bank[G, i] = bank(tag)
            l_codes, l_scales = lr_mx["l"]
            r_codes, r_scales = lr_mx["r"]
            cols = slice(i * P, (i + 1) * P)
            for t in range(SLOTS):
                rows = slice(G * HALF + t * P, G * HALF + (t + 1) * P)
                for B in range(2):
                    mx_pass(
                        plane_bank[G, i][:, t * P : (t + 1) * P],
                        r_codes[:, B, rows],
                        r_scales[:, B, rows],
                        l_codes[:, B, cols],
                        l_scales[:, B, cols],
                        B,
                    )

        def plane_copy(G, i, engine):
            at = (i % 4) * P
            copy_times_hebb(
                engine,
                out=plane_tile(G, i // 4)[:, at : at + P, :],
                in_=plane_bank[G, i][:].rearrange("p (t a) -> p a t", t=SLOTS),
            )

        rounded = {}

        def round_rows(i, h, engine):
            rounded[i, h] = work.tile([P, HALF], BF16, name=f"rounded{i}{h}", tag="rounded", bufs=4)
            copy(engine, out=rounded[i, h][:], in_=rows_sb[i, h][:])

        def transpose_out(G, pair, tag):
            plane_bank["pair", G, pair] = bank(tag)
            for a in range(2):
                words = rounded[2 * pair + a, G][:].bitcast(F32)
                for u in range(2):
                    at = (2 * a + u) * P
                    nc.tensor.transpose(plane_bank["pair", G, pair][:, at : at + P], words[:, u:256:2], ident[:])

        def plane_from_rows(G, pair, engine):
            words = plane_tile(G, pair // 2)[:].rearrange("p a t -> p (a t)").bitcast(F32)
            at = (pair % 2) * HALF
            copy(
                engine,
                out=words[:, at : at + HALF].rearrange("p (i a u) -> p i a u", i=2, u=2),
                in_=plane_bank["pair", G, pair][:].rearrange("p (i u a) -> p i a u", i=2, u=2),
            )

        def planes_out(G, e):
            cols = slice(e * HALF, (e + 1) * HALF)
            words = work.tile([P, HALF], U32, name=f"words{G}{e}", tag="words", bufs=4, align_bytes=64)
            nc.vector.quantize_mx(
                out=words[:].bitcast(FP8),
                scales=plane_scales[G][:, cols],
                in_=plane_in[G, e][:].rearrange("p a t -> p (a t)"),
            )
            nc.sync.dma_start(
                out=out_1[G].rearrange("p a t -> p (a t)")[:, e * 4 * HALF : (e + 1) * 4 * HALF].bitcast(I32),
                in_=words[:].bitcast(I32),
            )
            for Q in range(4):
                nc.sync.dma_start(
                    out=out_2[G, 4 * Q : 4 * Q + 4, cols].bitcast(I32),
                    in_=plane_scales[G][32 * Q : 32 * Q + 4, cols].bitcast(I32),
                )

        factors_ready()
        transpose_rows("q", 0, 0, 2)
        group_rows("q", 0, 0, 2, SCALAR)
        transpose_rows("q", 0, 2, 4)
        group_rows("q", 0, 3, 4, VECTOR)
        quantise_rows("q", 0, 0)
        group_rows("q", 0, 2, 3, SCALAR)
        quantise_rows("q", 0, 1)
        transpose_rows("g", 0, 0, 2)
        group_rows("g", 0, 0, 1, SCALAR)
        group_rows("g", 0, 1, 2, VECTOR)
        group_m0(0, 0, SCALAR)
        transpose_rows("g", 0, 2, 4)
        group_rows("g", 0, 3, 4, SCALAR)
        quantise_rows("g", 0, 0)
        products_gate(0, 0, 2)
        group_m0(0, 1, VECTOR)
        quantise_m0(0, 0)
        quantise_m0(0, 1)
        products_tanh(0, 0, 2)
        group_rows("g", 0, 2, 3, SCALAR)
        tanhs(0, 0, 2)
        times_s(0, 0, 2)
        quantise_rows("g", 0, 1)
        products_gate(0, 2, 4)
        gate(0, 0, 2)
        gate(0, 2, 4)
        products_tanh(0, 2, 4)
        transpose_rows("g", 1, 0, 2)
        group_rows("g", 1, 1, 2, VECTOR)
        tanhs(0, 2, 4)
        times_s(0, 2, 4)
        join_l(0)
        sum_for_r(0)
        group_rows("g", 1, 0, 1, SCALAR)
        quantise_rows("g", 1, 0)
        transpose_rows("g", 1, 2, 4)
        group_rows("g", 1, 2, 4, SCALAR)
        quantise_rows("g", 1, 1)
        scale_r(0)
        transpose_rows("q", 1, 0, 2)
        group_rows("q", 1, 1, 2, SCALAR)
        group_rows("q", 1, 0, 1, SCALAR)
        products_gate(1, 0, 2)
        quantise_rows("q", 1, 0)
        gate(1, 0, 2)
        group_m0(1, 0, SCALAR)
        transpose_rows("q", 1, 2, 4)
        products_gate(1, 2, 4)
        products_tanh(1, 0, 2)
        group_rows("q", 1, 3, 4, SCALAR)
        gate(1, 2, 4)
        group_rows("q", 1, 2, 3, SCALAR)
        tanhs(1, 0, 2)
        times_s(1, 0, 2)
        quantise_rows("q", 1, 1)
        products_gate(2, 0, 2)
        gate(2, 0, 2)
        quantise_lr("r", 0)
        products_tanh(1, 2, 4)
        tanhs(1, 2, 4)
        times_s(1, 2, 4)
        times_ratio(1, "sp", 2, 4)
        quantise_lr("l", 0)
        group_m0(1, 1, VECTOR)
        quantise_m0(1, 0)
        products_gate(2, 2, 4)
        quantise_m0(1, 1)
        gate(2, 2, 4)
        times_ratio(1, "sph", 2, 4)
        products_gate(3, 0, 2)
        products_tanh(2, 0, 2)
        times_ratio(1, "sph", 0, 2)
        join_l(1)
        times_ratio(1, "sp", 0, 2)
        products_tanh(2, 2, 4)
        tanhs(2, 0, 2)
        join_r(1)
        products_tanh(3, 0, 2)
        products_gate(3, 2, 4)
        gate(3, 0, 2)
        tanhs(2, 2, 4)
        times_s(2, 2, 4)
        quantise_lr("r", 1)
        times_s(2, 0, 2)
        tanhs(3, 0, 2)
        times_s(3, 0, 2)
        products_tanh(3, 2, 4)
        tanhs(3, 2, 4)
        times_s(3, 2, 4)
        times_ratio(3, "sph", 2, 4)
        quantise_lr("l", 1)
        rows_product(1, 0, "turn")
        plane_product(0, 3, "gate")
        times_ratio(3, "sp", 0, 2)
        gate(3, 2, 4)
        rows_product(2, 0, "turn")
        plane_product(0, 0, "gate")
        rows_product(0, 0, "tanh")
        join_l(2)
        plane_product(0, 2, "tanh")
        times_ratio(3, "sph", 0, 2)
        plane_product(0, 1, "turn")
        rows_out(1, 0, SCALAR)
        sum_for_r(2)
        plane_copy(0, 2, SCALAR)
        times_ratio(3, "sp", 2, 4)
        scale_r(2)
        quantise_lr("r", 2)
        rows_out(2, 0, SCALAR)
        plane_copy(0, 3, SCALAR)
        rows_product(3, 0, "turn")
        plane_copy(0, 1, SCALAR)
        quantise_lr("l", 2)
        rows_pass(5, 0, 0, "turn")
        rows_out(0, 0, SCALAR)
        plane_copy(0, 0, SCALAR)
        rows_pass(4, 0, 0, "gate")
        join_r(3)
        rows_pass(6, 0, 0, "gate")
        quantise_lr("r", 3)
        rows_product(2, 1, "tanh")
        rows_out(3, 0, SCALAR)
        rows_out(2, 1, SCALAR)
        rows_product(1, 1, "gate")
        rows_product(0, 1, "tanh")
        rows_out(0, 1, SCALAR)
        rows_out(1, 1, SCALAR)
        plane_product(1, 1, "tanh")
        join_l(3)
        plane_product(1, 2, "tanh")
        quantise_lr("l", 3)
        rows_product(7, 0, "turn")
        planes_out(0, 0)
        rows_pass(5, 0, 1)
        rows_out(5, 0, VECTOR)
        rows_pass(6, 0, 1)
        rows_out(7, 0, SCALAR)
        round_rows(7, 0, VECTOR)
        rows_pass(4, 0, 1)
        plane_copy(1, 2, VECTOR)
        plane_product(1, 3, "tanh")
        plane_product(1, 0, "turn")
        rows_product(7, 1, "tanh")
        plane_copy(1, 1, SCALAR)
        rows_out(6, 0, SCALAR)
        round_rows(6, 0, VECTOR)
        rows_product(6, 1, "tanh")
        plane_copy(1, 3, SCALAR)
        rows_product(4, 1, "turn")
        plane_copy(1, 0, VECTOR)
        round_rows(5, 0, VECTOR)
        rows_out(4, 0, SCALAR)
        planes_out(1, 0)
        round_rows(4, 0, SCALAR)
        rows_product(5, 1, "gate")
        rows_out(5, 1, VECTOR)
        transpose_out(0, 3, "turn")
        plane_from_rows(0, 3, VECTOR)
        rows_out(7, 1, SCALAR)
        transpose_out(0, 2, "gate")
        rows_out(6, 1, VECTOR)
        plane_from_rows(0, 2, SCALAR)
        planes_out(0, 1)
        plane_product(1, 6, "tanh")
        plane_product(1, 7, "tanh")
        plane_copy(1, 7, VECTOR)
        plane_copy(1, 6, SCALAR)
        rows_out(4, 1, SCALAR)
        plane_product(1, 5, "gate")
        plane_product(1, 4, "gate")
        plane_copy(1, 5, VECTOR)
        plane_copy(1, 4, VECTOR)
        rows_product(3, 1, "gate")
        rows_out(3, 1, SCALAR)
        planes_out(1, 1)
